import numpy as np
import ml_dtypes


def mxq(x, axis, fmt="e4m3"):
    dtype, down = {"e4m3": (ml_dtypes.float8_e4m3fn, 7), "e5m2": (ml_dtypes.float8_e5m2, 14)}[fmt]
    v = np.moveaxis(np.asarray(x, np.float32).astype(ml_dtypes.bfloat16).astype(np.float64), axis, -1)
    blocks = v.reshape(v.shape[:-1] + (-1, 32))
    amax = np.abs(blocks).max(-1, keepdims=True)
    byte = np.maximum(np.where(amax > 0, np.frexp(amax)[1] - 1 + 127, 0) - down, 1)
    scale = np.exp2(byte - 127.0)
    codes = (blocks / scale).astype(np.float32).astype(dtype).astype(np.float64)
    return np.moveaxis((codes * scale).reshape(v.shape), -1, axis)


WIDE = False


def mx_kscale(k):
    if not WIDE:
        return np.ones(k)
    levels = np.array([10, -10, 5, -5, 0])
    if k % 512:
        return np.exp2(np.random.permutation(np.resize(levels, k // 32))).repeat(32)
    a = np.empty((k // 512, 16))
    for p in range(k // 512):
        a[p, :8] = np.random.permutation(np.resize(levels, 8))
        for g in range(8):
            far = levels[np.abs(levels - a[p, g]) >= 10]
            a[p, g + 8] = far[np.random.randint(len(far))]
    return np.exp2(a.ravel()).repeat(32)


BF16 = ml_dtypes.bfloat16


def bf(x):
    return np.asarray(x, np.float32).astype(BF16)


def f64(x):
    return np.asarray(x).astype(np.float64)


E2M1 = np.array([0.0, 0.5, 1.0, 1.5, 2.0, 3.0, 4.0, 6.0, -0.0, -0.5, -1.0, -1.5, -2.0, -3.0, -4.0, -6.0])


def pack_weight(w, fmt):
    k, n = w.shape
    w = f64(bf(w)).reshape(k // 32, 32, n)
    amax = np.abs(w).max(1)
    if fmt == "e4m3":
        byte = np.frexp(amax)[1] - 1 + 127 - 7
    else:
        mant, ex = np.frexp(amax / 6.0)
        byte = np.where(mant > 0.5, ex, ex - 1) + 127
    byte = np.clip(np.where(amax > 0, byte, 1), 1, 254)
    scaled = (w * np.exp2(127.0 - byte)[:, None, :]).reshape(k, n).astype(np.float32)
    by_word = np.ascontiguousarray(scaled.reshape(k // 512, 128, 4, n).transpose(0, 1, 3, 2))
    if fmt == "e4m3":
        words = by_word.astype(ml_dtypes.float8_e4m3fn).view(np.uint8)
    else:
        c = by_word.astype(ml_dtypes.float4_e2m1fn).view(np.uint8) & 0xF
        words = c[..., 0::2] | (c[..., 1::2] << 4)
    return np.ascontiguousarray(words), np.ascontiguousarray(byte.astype(np.uint8).reshape(k // 512, 16, n))


def unpack_weight(words, scales, fmt):
    g, p, n, _ = words.shape
    if fmt == "e4m3":
        vals = np.ascontiguousarray(words).view(ml_dtypes.float8_e4m3fn).astype(np.float64)
    else:
        nib = np.empty((g, p, n, 4), np.uint8)
        nib[..., 0::2] = words & 0xF
        nib[..., 1::2] = words >> 4
        vals = E2M1[nib]
    vals = vals * np.repeat(np.exp2(scales.astype(np.float64) - 127.0), 8, axis=1)[..., None]
    return vals.transpose(0, 1, 3, 2).reshape(g * 512, n)
def pack4(w):
    words, scales = pack_weight(w, "e2m1")
    return words.reshape(words.shape[0], 128, -1), scales


def unpack4(words, scales):
    return unpack_weight(words.reshape(words.shape[0], 128, -1, 2), scales, "e2m1")


M, K, P, N = 512, 1024, 512, 1024


def sigmoid(v):
    return 1.0 / (1.0 + np.exp(-v))


def draw0():
    s, u, t = mx_kscale(K), mx_kscale(P), mx_kscale(N)
    wx_words, wx_scales = pack4(np.random.standard_normal((K, 4 * N)) / np.sqrt(K) / s[:, None])
    wr_words, wr_scales = pack4(np.random.standard_normal((P, 4 * N)) / np.sqrt(P) / u[:, None])
    wp_words, wp_scales = pack4(np.random.standard_normal((N, P)) / np.sqrt(N) / t[:, None])
    return {"x": bf(np.random.standard_normal((M, K)) * s),
            "r_prev": bf(np.random.standard_normal((M, P)) * u),
            "c_prev": bf(np.random.standard_normal((M, N))),
            "wx_words": wx_words, "wx_scales": wx_scales,
            "wr_words": wr_words, "wr_scales": wr_scales,
            "bias": bf(0.5 * np.random.standard_normal(4 * N)),
            "peep": bf(0.5 * np.random.standard_normal((3, N))),
            "hscale": bf((1.0 + 0.1 * np.random.standard_normal(N)) * t),
            "wp_words": wp_words, "wp_scales": wp_scales}


def core(x, r_prev, c_prev, wx_words, wx_scales, wr_words, wr_scales, bias, peep, hscale, wp_words, wp_scales):
    wx = unpack4(wx_words, wx_scales)
    wr = unpack4(wr_words, wr_scales)
    wp = unpack4(wp_words, wp_scales)
    cp = f64(c_prev)
    pe = f64(peep)
    zx = mxq(f64(x), 1, "e4m3") @ wx
    zr = mxq(f64(r_prev), 1, "e4m3") @ wr
    z = zx + zr + f64(bias)
    gi = sigmoid(z[:, :N] + pe[0] * cp)
    gf = sigmoid(z[:, N:2 * N] + pe[1] * cp)
    cand = np.tanh(z[:, 2 * N:3 * N])
    c = gf * cp + gi * cand
    go = sigmoid(z[:, 3 * N:] + pe[2] * c)
    h = go * np.tanh(c) * f64(hscale)
    r = mxq(h, 1, "e4m3") @ wp
    return r, c


def e4m3fn_bytes(y):
    return np.clip(np.asarray(y, np.float64), -448.0, 448.0).astype(np.float32).astype(ml_dtypes.float8_e4m3fn).view(np.uint8)


def e4m3fn_values(b):
    return np.asarray(b, np.uint8).view(ml_dtypes.float8_e4m3fn).astype(np.float64)


def setup_inputs():
    d = draw0()
    x0 = np.asarray(d['x']).astype(np.float64)
    s = (np.max(np.abs(x0), axis=(0,), keepdims=True) / 448.0).astype(np.float32)
    out = {}
    for k, v in d.items():
        if k == 'x':
            out['x_bytes'] = e4m3fn_bytes(x0 / s.astype(np.float64))
            out['x_scale'] = s
        else:
            out[k] = v
    return out


def reference(x_bytes, x_scale, r_prev, c_prev, wx_words, wx_scales, wr_words, wr_scales, bias, peep, hscale, wp_words, wp_scales):
    return core(e4m3fn_values(x_bytes) * x_scale.astype(np.float64), r_prev, c_prev, wx_words, wx_scales, wr_words, wr_scales, bias, peep, hscale, wp_words, wp_scales)

@@ -1,0 +1,444 @@
+from contextlib import ExitStack
+
+import concourse.mybir as mybir
+from concourse.masks import make_identity
+
+M, K, R, N = 512, 1024, 512, 1024
+FLOPS = 2 * M * (K + R) * 4 * N + 2 * M * N * R
+
+F32 = mybir.dt.float32
+BF16 = mybir.dt.bfloat16
+U32 = mybir.dt.uint32
+I32 = mybir.dt.int32
+U8 = mybir.dt.uint8
+FP8 = mybir.dt.float8_e4m3fn
+FP8X4 = mybir.dt.float8_e4m3fn_x4
+FP4X4 = mybir.dt.float4_e2m1fn_x4
+ALU = mybir.AluOpType
+ACT = mybir.ActivationFunctionType
+
+P = 128
+GI, GF, GA, GO = 0, 1, 2, 3
+
+UNITS = [(0, 0, 256), (0, 256, 256)] + [(c, 0, 512) for c in range(1, 7)] + [(7, 0, 256), (7, 256, 256)]
+
+
+def tile_lstmp_peephole_step_f1_kernel(
+    tc, x_bytes, x_scale, r_prev, c_prev, wx_words, wx_scales, wr_words, wr_scales, bias, peep, hscale, wp_words, wp_scales, out_r, out_c
+):
+    nc = tc.nc
+    with ExitStack() as ctx:
+        keep = ctx.enter_context(tc.tile_pool(name="keep", bufs=1))
+        work = ctx.enter_context(tc.tile_pool(name="work", bufs=2))
+        psum = ctx.enter_context(tc.psum_pool(name="psum", bufs=1))
+
+        warm = keep.tile([P, 1], F32, name="warm")
+        xs = keep.tile([P, K], F32, name="xs")
+        xb = keep.tile([P, 4, K], U8, name="xb")
+        xv = keep.tile([P, 4, K], BF16, name="xv")
+        rv = keep.tile([P, 4, R], BF16, name="rv")
+        grouped = keep.tile([P, 3, M, 4], BF16, name="grouped", align_bytes=64)
+        codes = keep.tile([P, 3, M], U32, name="codes", align_bytes=64)
+        scales = keep.tile([P, 3, M], U8, name="scales", align_bytes=64)
+        rows = keep.tile([P, P], BF16, name="rows")
+        cols = keep.tile([P, 64], F32, name="cols")
+        ident_f = keep.tile([P, P], F32, name="ident_f")
+        ident_b = keep.tile([P, P], BF16, name="ident_b")
+        sel = keep.tile([P, 4, P], BF16, name="sel")
+        planes = keep.tile([P, 3 * 4 * N], U8, name="planes", align_bytes=64)
+        pplanes = keep.tile([P, 2 * R], U8, name="pplanes", align_bytes=64)
+        words = keep.tile([P, 3, 4, 2 * N], U8, name="words", align_bytes=64)
+        pwords = keep.tile([P, 2, 2 * R], U8, name="pwords", align_bytes=64)
+        cp = keep.tile([P, 4, N], BF16, name="cp")
+        cpt = keep.tile([P, 8, M], BF16, name="cpt")
+        hp = keep.tile([P, 2, 4, M], BF16, name="hp")
+        hg = keep.tile([P, 2, M, 4], BF16, name="hg", align_bytes=64)
+        hcodes = keep.tile([P, 2, M], U32, name="hcodes", align_bytes=64)
+        hscales = keep.tile([P, 2, M], U8, name="hscales", align_bytes=64)
+
+        nc.vector.memset(warm[:], 0.0)
+        nc.scalar.activation(out=warm[:], in_=warm[:], func=ACT.Sigmoid)
+        xb_src = x_bytes.rearrange("(t p) k -> p t k", p=P)
+        rv_src = r_prev.rearrange("(t p) k -> p t k", p=P)
+        cp_src = c_prev.rearrange("(t p) k -> p t k", p=P)
+        xs_row = x_scale.rearrange("o k -> (o k)")
+        planes_i = planes[:].bitcast(I32)
+        pplanes_i = pplanes[:].bitcast(I32)
+        wx_s = wx_scales.bitcast(I32)
+        wr_s = wr_scales.bitcast(I32)
+        wp_s = wp_scales.bitcast(I32)
+        Q4 = N
+
+        nc.gpsimd.memset(rows[:], 0.0)
+        nc.vector.memset(planes_i[:, 0 : 2 * Q4], 0)
+        nc.vector.memset(planes_i[:, 2 * Q4 : 3 * Q4], 0)
+
+        def load_words(c0, c1):
+            a, b = 2 * c0, 2 * c1
+            for g, src in ((2, wr_words[0]), (0, wx_words[0]), (1, wx_words[1])):
+                nc.sync.dma_start(out=words[:, g, :, a:b], in_=src.rearrange("p (q n) -> p q n", q=4)[:, :, a:b])
+
+        def load_cp(c0, c1):
+            nc.sync.dma_start(out=cp[:, :, c0:c1], in_=cp_src[:, :, c0:c1])
+
+        nc.gpsimd.dma_start(out=rows[0:32, :], in_=bias.rearrange("(a b) -> a b", b=P))
+        nc.gpsimd.dma_start(out=rows[32:56, :], in_=peep.rearrange("g (a b) -> (g a) b", b=P))
+        nc.gpsimd.dma_start(out=rows[56:64, :], in_=hscale.rearrange("(a b) -> a b", b=P))
+        nc.gpsimd.dma_start(out=cp[:, :, 0:256], in_=cp_src[:, :, 0:256])
+        nc.scalar.dma_start(out=xs[:, 0:512], in_=xs_row[0:512].partition_broadcast(P))
+        nc.sync.dma_start(out=xb[:, 0:2, :], in_=xb_src[:, 0:2, :])
+        nc.scalar.dma_start(out=xs[:, 512:1024], in_=xs_row[512:1024].partition_broadcast(P))
+        nc.sync.dma_start(out=rv[:], in_=rv_src)
+        load_words(0, 128)
+        nc.sync.dma_start(out=xb[:, 2:4, :], in_=xb_src[:, 2:4, :])
+        for r in range(4):
+            nc.sync.dma_start(
+                out=planes_i[r:P:32, 0 : 2 * Q4].rearrange("p (g n) -> p g n", g=2),
+                in_=wx_s[:, r:16:4, :].rearrange("g q n -> q g n"),
+            )
+        for r in range(4):
+            nc.sync.dma_start(out=planes_i[r:P:32, 2 * Q4 : 3 * Q4], in_=wr_s[0, r:16:4, :])
+        load_words(128, 256)
+        load_words(256, 512)
+        load_cp(256, 1024)
+        load_words(512, 1024)
+        make_identity(nc, ident_f[:])
+        make_identity(nc, ident_b[:])
+        nc.gpsimd.memset(pplanes_i[:], 0)
+        nc.gpsimd.memset(sel[:], 0.0)
+        nc.gpsimd.tensor_copy(out=sel[:, :, 96:128], in_=ident_b[:].rearrange("p (i t) -> p t i", t=4))
+        for r in range(4):
+            nc.sync.dma_start(
+                out=pplanes_i[r:P:32, :].rearrange("p (g n) -> p g n", g=2),
+                in_=wp_s[:, r:16:4, :].rearrange("g q n -> q g n"),
+            )
+        nc.sync.dma_start(out=pwords[:], in_=wp_words.rearrange("g p n -> p g n"))
+
+        def z_tile(shape, dtype, name):
+            return psum.tile(shape, dtype, name=name, tag="z", bufs=6)
+
+        def t_tile(shape, dtype, name):
+            return psum.tile(shape, dtype, name=name, tag="t", bufs=2)
+
+        def col(i):
+            return cols[:, i : i + 1]
+
+        def bias_col(gate, c):
+            return col(8 * gate + c)
+
+        def peep_col(j, c):
+            return col(32 + 8 * j + c)
+
+        def hs_col(c):
+            return col(56 + c)
+
+        def product(t, g):
+            ks = slice(512 * g, 512 * g + 512)
+            nc.vector.tensor_tensor(out=xv[:, t, ks], in0=xb[:, t, ks].bitcast(FP8), in1=xs[:, ks], op=ALU.mult)
+
+        def turn(src, g, word0, half):
+            bank = z_tile([P, 2, 2, P], F32, "turn")
+            for i in range(2):
+                w = src[:, 2 * half + i, :].bitcast(F32)
+                for u in range(2):
+                    nc.tensor.transpose(bank[:, i, u, :], w[:, word0 + u : word0 + 256 : 2], ident_f[:])
+            return bank
+
+        def untangle(bank, g, half):
+            dst = grouped[:, g, 256 * half : 256 * half + 256, :].rearrange("p n t -> p (n t)").bitcast(F32)
+            dst = dst.rearrange("p (i r u) -> p i r u", i=2, u=2)
+            nc.scalar.copy(out=dst, in_=bank[:].rearrange("p i u r -> p i r u"))
+
+        def quantize(g, half):
+            ts = slice(256 * half, 256 * half + 256)
+            nc.vector.quantize_mx(
+                out=codes[:, g, ts].bitcast(FP8X4),
+                scales=scales[:, g, ts],
+                in_=grouped[:, g, ts, :].rearrange("p n t -> p (n t)"),
+            )
+
+        def gate_matmuls(gate, c, t0, tn):
+            z = z_tile([P, tn], F32, "z")
+            n0 = gate * N + P * c
+            step = 512 if tn == 512 else 128
+            for s0 in range(0, tn, step):
+                ts = slice(t0 + s0, t0 + s0 + step)
+                for j, g in enumerate((2, 0, 1)):
+                    nc.tensor.matmul_mx(
+                        out=z[:, s0 : s0 + step],
+                        lhsT=words[:, g, gate, 2 * P * c : 2 * P * (c + 1)].bitcast(FP4X4),
+                        lhsT_scale=planes[:, g * 4 * N + n0 : g * 4 * N + n0 + P],
+                        rhs=codes[:, g, ts].bitcast(FP8X4),
+                        rhs_scale=scales[:, g, ts],
+                        start=(j == 0),
+                        stop=(j == 2),
+                    )
+            return z
+
+        def turn_cp(c):
+            bank = t_tile([P, M], BF16, "cp_bank")
+            for t in range(4):
+                nc.tensor.transpose(bank[:, P * t : P * (t + 1)], cp[:, t, P * c : P * (c + 1)], ident_b[:])
+            return bank
+
+        def keep_cp(c, bank):
+            nc.scalar.copy(out=cpt[:, c, :], in_=bank[:])
+
+        def w_tile(name, tn, dtype=F32, bufs=2):
+            return work.tile([P, tn], dtype, name=name, tag=name, bufs=bufs)
+
+        state = {}
+        c_rows = {}
+        last = len(UNITS) - 1
+
+        def matmuls(u, gates=(GF, GI, GA, GO)):
+            c, t0, tn = UNITS[u]
+            for gate in gates:
+                state.setdefault(u, {})[gate] = gate_matmuls(gate, c, t0, tn)
+
+        def v_uf(u):
+            c, t0, tn = UNITS[u]
+            st = state[u]
+            st["uf"] = w_tile("uf", tn)
+            nc.vector.scalar_tensor_tensor(out=st["uf"][:], in0=cpt[:, c, t0 : t0 + tn], scalar=peep_col(1, c), in1=st[GF][:], op0=ALU.mult, op1=ALU.add)
+
+        def v_ui(u):
+            c, t0, tn = UNITS[u]
+            st = state[u]
+            st["ui"] = w_tile("ui", tn)
+            nc.vector.scalar_tensor_tensor(out=st["ui"][:], in0=cpt[:, c, t0 : t0 + tn], scalar=peep_col(0, c), in1=st[GI][:], op0=ALU.mult, op1=ALU.add)
+
+        def v_uo(u):
+            c, t0, tn = UNITS[u]
+            st = state[u]
+            st["uo"] = w_tile("uo", tn)
+            nc.vector.scalar_tensor_tensor(out=st["uo"][:], in0=st["c"][:], scalar=peep_col(2, c), in1=st[GO][:], op0=ALU.mult, op1=ALU.add)
+
+        def v_fc(u):
+            c, t0, tn = UNITS[u]
+            st = state[u]
+            st["fc"] = w_tile("fc", tn)
+            nc.vector.tensor_tensor(out=st["fc"][:], in0=st["f"][:], in1=cpt[:, c, t0 : t0 + tn], op=ALU.mult)
+
+        def v_ia(u):
+            c, t0, tn = UNITS[u]
+            st = state[u]
+            st["ia"] = w_tile("ia", tn)
+            nc.vector.tensor_tensor(out=st["ia"][:], in0=st["i"][:], in1=st["a"][:], op=ALU.mult)
+
+        def v_c(u):
+            c, t0, tn = UNITS[u]
+            st = state[u]
+            st["c"] = w_tile("cn", tn, bufs=3)
+            nc.vector.tensor_tensor(out=st["c"][:], in0=st["fc"][:], in1=st["ia"][:], op=ALU.add)
+
+        def v_h(u):
+            c, t0, tn = UNITS[u]
+            st = state[u]
+            h = w_tile("h", tn, BF16, bufs=3)
+            nc.vector.scalar_tensor_tensor(out=h[:], in0=st["o"][:], scalar=hs_col(c), in1=st["tanh"][:], op0=ALU.mult, op1=ALU.mult)
+            st["h"] = h
+            g, j = c // 4, c % 4
+            if u == last:
+                return
+            for t in range(4):
+                nc.sync.dma_start(out=hp[32 * j : 32 * j + 32, g, t, t0 : t0 + tn], in_=h[t:P:4, :])
+
+        def s_act(u, key, src, func, gate):
+            c, t0, tn = UNITS[u]
+            st = state[u]
+            st[key] = w_tile(key, tn)
+            nc.scalar.activation(out=st[key][:], in_=st[src][:], func=func, bias=bias_col(gate, c))
+
+        def s_a(u):
+            s_act(u, "a", GA, ACT.Tanh, GA)
+
+        def s_f(u):
+            s_act(u, "f", "uf", ACT.Sigmoid, GF)
+
+        def s_i(u):
+            s_act(u, "i", "ui", ACT.Sigmoid, GI)
+
+        def s_o(u):
+            s_act(u, "o", "uo", ACT.Sigmoid, GO)
+
+        def s_tanh(u):
+            c, t0, tn = UNITS[u]
+            st = state[u]
+            st["tanh"] = w_tile("tanh", tn)
+            nc.scalar.activation(out=st["tanh"][:], in_=st["c"][:], func=ACT.Tanh)
+
+        def turn_c(u):
+            c, t0, tn = UNITS[u]
+            bank = t_tile([P, tn // P, P], F32, "c_bank")
+            for i in range(tn // P):
+                nc.tensor.transpose(bank[:, i, :], state[u]["c"][:, P * i : P * (i + 1)], ident_f[:])
+            state[u]["bank"] = bank
+
+        def store_c(u):
+            c, t0, tn = UNITS[u]
+            rs = slice(t0 // P, (t0 + tn) // P)
+            if c % 2 == 0 and t0 == 0:
+                c_rows[0] = work.tile([P, 4, 2 * P], F32, name="c_rows", tag="c_rows", bufs=2)
+            dst = c_rows[0]
+            a = P * (c % 2)
+            nc.scalar.copy(out=dst[:, rs, a : a + P], in_=state[u]["bank"][:])
+            if c % 2 == 1:
+                nc.sync.dma_start(
+                    out=out_c.rearrange("(t p) n -> p t n", p=P)[:, rs, P * (c - 1) : P * (c + 1)],
+                    in_=dst[:, rs, :],
+                )
+
+        def group_h(g, t0, tn, engine, p1=P):
+            dst = hg[0:p1, g, t0 : t0 + tn, :].rearrange("p (n i) t -> p n t i", i=4)
+            src = hp[0:p1, g, :, t0 : t0 + tn].rearrange("p t (n i) -> p n t i", i=4)
+            if engine == "s":
+                nc.scalar.copy(out=dst, in_=src)
+            else:
+                nc.vector.tensor_copy(out=dst, in_=src)
+
+        def turn_h(t0):
+            h = state[last]["h"]
+            a = t0 - UNITS[last][1]
+            bank = t_tile([P, 4, P], BF16, "h_bank")
+            for t in range(4):
+                nc.tensor.matmul(out=bank[:, t, :], lhsT=sel[:, t, :], rhs=h[:, a : a + P], start=True, stop=True)
+            return bank
+
+        def untangle_h(t0, bank, engine):
+            dst = hg[96:P, 1, t0 : t0 + P, :]
+            src = bank[96:P, :, :].rearrange("p t n -> p n t")
+            if engine == "s":
+                nc.scalar.copy(out=dst, in_=src)
+            else:
+                nc.vector.tensor_copy(out=dst, in_=src)
+
+        def quantize_h(g, t0, tn):
+            ts = slice(t0, t0 + tn)
+            nc.vector.quantize_mx(
+                out=hcodes[:, g, ts].bitcast(FP8X4),
+                scales=hscales[:, g, ts],
+                in_=hg[:, g, ts, :].rearrange("p n t -> p (n t)"),
+            )
+
+        def project(t):
+            z = z_tile([P, R], F32, "r")
+            ts = slice(P * t, P * (t + 1))
+            for g in range(2):
+                nc.tensor.matmul_mx(
+                    out=z[:],
+                    lhsT=hcodes[:, g, ts].bitcast(FP8X4),
+                    lhsT_scale=hscales[:, g, ts],
+                    rhs=pwords[:, g, :].bitcast(FP4X4),
+                    rhs_scale=pplanes[:, g * R : (g + 1) * R],
+                    start=(g == 0),
+                    stop=(g == 1),
+                )
+            return z
+
+        def store_r(t, z, engine):
+            r_sb = work.tile([P, R], F32, name="r_sb", tag="r_sb", bufs=4)
+            if engine == "v":
+                nc.vector.tensor_copy(out=r_sb[:], in_=z[:])
+            else:
+                nc.scalar.copy(out=r_sb[:], in_=z[:])
+            nc.sync.dma_start(out=out_r[P * t : P * (t + 1), :], in_=r_sb[:])
+
+        ctx.enter_context(tc.manual_schedule(engines={mybir.EngineType.PE, mybir.EngineType.DVE, mybir.EngineType.Activation}))
+
+        product(0, 0)
+        product(1, 0)
+        r0 = turn(rv, 2, 0, 0)
+        untangle(r0, 2, 0)
+        x00 = turn(xv, 0, 0, 0)
+        untangle(x00, 0, 0)
+        product(0, 1)
+        product(1, 1)
+        x01 = turn(xv, 1, 256, 0)
+        untangle(x01, 1, 0)
+        rows_bank = t_tile([P, P], BF16, "rows_bank")
+        nc.tensor.transpose(rows_bank[:], rows[:], ident_b[:])
+        nc.scalar.copy(out=cols[:], in_=rows_bank[:, 0:64])
+        product(2, 0)
+        product(3, 0)
+        quantize(2, 0)
+        quantize(0, 0)
+        quantize(1, 0)
+        x10 = turn(xv, 0, 0, 1)
+        untangle(x10, 0, 1)
+        product(2, 1)
+        product(3, 1)
+        matmuls(0, (GF, GI))
+        b0 = turn_cp(0)
+        keep_cp(0, b0)
+        matmuls(0, (GA, GO))
+        r1 = turn(rv, 2, 0, 1)
+        untangle(r1, 2, 1)
+        x11 = turn(xv, 1, 256, 1)
+        untangle(x11, 1, 1)
+        b1 = turn_cp(1)
+
+        def step(u, before=None, turns=()):
+            v_uf(u)
+            s_a(u)
+            v_ui(u)
+            if u > 0:
+                s_tanh(u - 1)
+            s_f(u)
+            s_i(u)
+            if before is not None:
+                before()
+            if u < last:
+                matmuls(u + 1, (GF, GI))
+            if u > 0:
+                turn_c(u - 1)
+                v_uo(u - 1)
+                s_o(u - 1)
+            banks = [(c, turn_cp(c)) for c in turns]
+            if u < last:
+                matmuls(u + 1, (GA, GO))
+            v_fc(u)
+            v_ia(u)
+            if u > 0:
+                v_h(u - 1)
+                store_c(u - 1)
+            v_c(u)
+            for c, bank in banks:
+                keep_cp(c, bank)
+
+        def finish_x():
+            quantize(2, 1)
+            quantize(0, 1)
+            quantize(1, 1)
+            keep_cp(1, b1)
+
+        for u in range(last + 1):
+            c, t0, tn = UNITS[u]
+            step(u, finish_x if u == 0 else None, [c + 1] if 1 <= c < 7 else [])
+            if u == 6:
+                group_h(0, 0, 256, "s")
+            if u == 7:
+                group_h(0, 256, 256, "s")
+                quantize_h(0, 0, 256)
+            if u == 8:
+                quantize_h(0, 256, 256)
+        s_tanh(last)
+        v_uo(last)
+        s_o(last)
+        turn_c(last)
+        group_h(1, 256, 256, "v", 96)
+        v_h(last)
+        store_c(last)
+        banks = [turn_h(256), turn_h(384)]
+        untangle_h(256, banks[0], "v")
+        untangle_h(384, banks[1], "s")
+        group_h(1, 0, 256, "v")
+        quantize_h(1, 256, 128)
+        quantize_h(1, 384, 128)
+        z = [project(2), project(3)]
+        quantize_h(1, 0, 256)
+        store_r(2, z[0], "s")
+        store_r(3, z[1], "v")
+        z = [project(0), project(1)]
+        store_r(0, z[0], "v")
+        store_r(1, z[1], "s")

@@ -20,6 +20,7 @@ ACT = mybir.ActivationFunctionType
 P = 128
 GI, GF, GA, GO = 0, 1, 2, 3
 
+ORDER = "xs0 xb0 xs1 rv0 rows xb1 w0 sx sr cp0 rv1 w1 w2 cp1 w3 cp2 wp"
 UNITS = [(0, 0, 256), (0, 256, 256)] + [(c, 0, 512) for c in range(1, 7)] + [(7, 0, 256), (7, 256, 256)]
 
 
@@ -47,11 +48,13 @@ def tile_lstmp_peephole_step_f1_kernel(
         sel = keep.tile([P, 4, P], BF16, name="sel")
         planes = keep.tile([P, 3 * 4 * N], U8, name="planes", align_bytes=64)
         pplanes = keep.tile([P, 2 * R], U8, name="pplanes", align_bytes=64)
-        words = keep.tile([P, 3, 4, 2 * N], U8, name="words", align_bytes=64)
+        chunks = [(0, 128), (128, 256), (256, 512), (512, 1024)]
+        words = [keep.tile([P, 3, 4, 2 * (b - a)], U8, name="words_%d" % a, align_bytes=64) for a, b in chunks]
+        cp_chunks = [(0, 128), (128, 512), (512, 1024)]
         pwords = keep.tile([P, 2, 2 * R], U8, name="pwords", align_bytes=64)
-        cp = keep.tile([P, 4, N], BF16, name="cp")
+        cp = [keep.tile([P, 4, b - a], BF16, name="cp_%d" % a) for a, b in cp_chunks]
         cpt = keep.tile([P, 8, M], BF16, name="cpt")
-        hp = keep.tile([P, 2, 4, M], BF16, name="hp")
+        hp = keep.tile([P, 2, 2, 4, 256], BF16, name="hp")
         hg = keep.tile([P, 2, M, 4], BF16, name="hg", align_bytes=64)
         hcodes = keep.tile([P, 2, M], U32, name="hcodes", align_bytes=64)
         hscales = keep.tile([P, 2, M], U8, name="hscales", align_bytes=64)
@@ -69,50 +72,84 @@ def tile_lstmp_peephole_step_f1_kernel(
         wp_s = wp_scales.bitcast(I32)
         Q4 = N
 
-        nc.gpsimd.memset(rows[:], 0.0)
+        make_identity(nc, ident_f[:])
+        make_identity(nc, ident_b[:])
+        nc.gpsimd.memset(sel[:], 0.0)
+        nc.gpsimd.tensor_copy(out=sel[:, :, 96:128], in_=ident_b[:].rearrange("p (i t) -> p t i", t=4))
+        nc.gpsimd.memset(pplanes_i[:], 0)
+        nc.vector.memset(rows[:], 0.0)
         nc.vector.memset(planes_i[:, 0 : 2 * Q4], 0)
         nc.vector.memset(planes_i[:, 2 * Q4 : 3 * Q4], 0)
 
-        def load_words(c0, c1):
-            a, b = 2 * c0, 2 * c1
-            for g, src in ((2, wr_words[0]), (0, wx_words[0]), (1, wx_words[1])):
-                nc.sync.dma_start(out=words[:, g, :, a:b], in_=src.rearrange("p (q n) -> p q n", q=4)[:, :, a:b])
+        def load_words(i):
+            a, b = chunks[i]
+            for g in (2, 0, 1):
+                src = wr_words[0] if g == 2 else wx_words[g]
+                nc.sync.dma_start(out=words[i][:, g, :, :], in_=src.rearrange("p (q n) -> p q n", q=4)[:, :, 2 * a : 2 * b])
 
-        def load_cp(c0, c1):
-            nc.sync.dma_start(out=cp[:, :, c0:c1], in_=cp_src[:, :, c0:c1])
+        def load_cp(i):
+            a, b = cp_chunks[i]
+            nc.sync.dma_start(out=cp[i][:], in_=cp_src[:, :, a:b])
 
-        nc.gpsimd.dma_start(out=rows[0:32, :], in_=bias.rearrange("(a b) -> a b", b=P))
-        nc.gpsimd.dma_start(out=rows[32:56, :], in_=peep.rearrange("g (a b) -> (g a) b", b=P))
-        nc.gpsimd.dma_start(out=rows[56:64, :], in_=hscale.rearrange("(a b) -> a b", b=P))
-        nc.gpsimd.dma_start(out=cp[:, :, 0:256], in_=cp_src[:, :, 0:256])
-        nc.scalar.dma_start(out=xs[:, 0:512], in_=xs_row[0:512].partition_broadcast(P))
-        nc.sync.dma_start(out=xb[:, 0:2, :], in_=xb_src[:, 0:2, :])
-        nc.scalar.dma_start(out=xs[:, 512:1024], in_=xs_row[512:1024].partition_broadcast(P))
-        nc.sync.dma_start(out=rv[:], in_=rv_src)
-        load_words(0, 128)
-        nc.sync.dma_start(out=xb[:, 2:4, :], in_=xb_src[:, 2:4, :])
-        for r in range(4):
-            nc.sync.dma_start(
-                out=planes_i[r:P:32, 0 : 2 * Q4].rearrange("p (g n) -> p g n", g=2),
-                in_=wx_s[:, r:16:4, :].rearrange("g q n -> q g n"),
-            )
-        for r in range(4):
-            nc.sync.dma_start(out=planes_i[r:P:32, 2 * Q4 : 3 * Q4], in_=wr_s[0, r:16:4, :])
-        load_words(128, 256)
-        load_words(256, 512)
-        load_cp(256, 1024)
-        load_words(512, 1024)
-        make_identity(nc, ident_f[:])
-        make_identity(nc, ident_b[:])
-        nc.gpsimd.memset(pplanes_i[:], 0)
-        nc.gpsimd.memset(sel[:], 0.0)
-        nc.gpsimd.tensor_copy(out=sel[:, :, 96:128], in_=ident_b[:].rearrange("p (i t) -> p t i", t=4))
-        for r in range(4):
-            nc.sync.dma_start(
-                out=pplanes_i[r:P:32, :].rearrange("p (g n) -> p g n", g=2),
-                in_=wp_s[:, r:16:4, :].rearrange("g q n -> q g n"),
-            )
-        nc.sync.dma_start(out=pwords[:], in_=wp_words.rearrange("g p n -> p g n"))
+        def chunk_of(ranges, c):
+            i = [k for k, (a, b) in enumerate(ranges) if a <= P * c < b][0]
+            return i, P * c - ranges[i][0]
+
+        def load_xs(a, b):
+            nc.scalar.dma_start(out=xs[:, a:b], in_=xs_row[a:b].partition_broadcast(P))
+
+        def load_xb(a, b):
+            nc.sync.dma_start(out=xb[:, a:b, :], in_=xb_src[:, a:b, :])
+
+        def load_rv(a, b):
+            nc.sync.dma_start(out=rv[:, a:b, :], in_=rv_src[:, a:b, :])
+
+        def load_rows():
+            nc.sync.dma_start(out=rows[0:32, :], in_=bias.rearrange("(a b) -> a b", b=P))
+            nc.sync.dma_start(out=rows[32:56, :], in_=peep.rearrange("g (a b) -> (g a) b", b=P))
+            nc.sync.dma_start(out=rows[56:64, :], in_=hscale.rearrange("(a b) -> a b", b=P))
+
+        def load_wx_scales():
+            for r in range(4):
+                nc.sync.dma_start(
+                    out=planes_i[r:P:32, 0 : 2 * Q4].rearrange("p (g n) -> p g n", g=2),
+                    in_=wx_s[:, r:16:4, :].rearrange("g q n -> q g n"),
+                )
+
+        def load_wr_scales():
+            for r in range(4):
+                nc.sync.dma_start(out=planes_i[r:P:32, 2 * Q4 : 3 * Q4], in_=wr_s[0, r:16:4, :])
+
+        def load_projection():
+            for r in range(4):
+                nc.sync.dma_start(
+                    out=pplanes_i[r:P:32, :].rearrange("p (g n) -> p g n", g=2),
+                    in_=wp_s[:, r:16:4, :].rearrange("g q n -> q g n"),
+                )
+            nc.sync.dma_start(out=pwords[:], in_=wp_words.rearrange("g p n -> p g n"))
+
+        loads = {
+            "xs0": lambda: load_xs(0, 512),
+            "xs1": lambda: load_xs(512, 1024),
+            "xb0": lambda: load_xb(0, 2),
+            "xb1": lambda: load_xb(2, 4),
+            "rv0": lambda: load_rv(0, 2),
+            "rv1": lambda: load_rv(2, 4),
+            "rv": lambda: load_rv(0, 4),
+            "rows": load_rows,
+            "sx": load_wx_scales,
+            "sr": load_wr_scales,
+            "w0": lambda: load_words(0),
+            "w1": lambda: load_words(1),
+            "w2": lambda: load_words(2),
+            "w3": lambda: load_words(3),
+            "cp0": lambda: load_cp(0),
+            "cp1": lambda: load_cp(1),
+            "cp2": lambda: load_cp(2),
+            "wp": load_projection,
+        }
+        for name in ORDER.split():
+            loads[name]()
 
         def z_tile(shape, dtype, name):
             return psum.tile(shape, dtype, name=name, tag="z", bufs=6)
@@ -160,13 +197,14 @@ def tile_lstmp_peephole_step_f1_kernel(
         def gate_matmuls(gate, c, t0, tn):
             z = z_tile([P, tn], F32, "z")
             n0 = gate * N + P * c
+            wi, w0 = chunk_of(chunks, c)
             step = 512 if tn == 512 else 128
             for s0 in range(0, tn, step):
                 ts = slice(t0 + s0, t0 + s0 + step)
                 for j, g in enumerate((2, 0, 1)):
                     nc.tensor.matmul_mx(
                         out=z[:, s0 : s0 + step],
-                        lhsT=words[:, g, gate, 2 * P * c : 2 * P * (c + 1)].bitcast(FP4X4),
+                        lhsT=words[wi][:, g, gate, 2 * w0 : 2 * (w0 + P)].bitcast(FP4X4),
                         lhsT_scale=planes[:, g * 4 * N + n0 : g * 4 * N + n0 + P],
                         rhs=codes[:, g, ts].bitcast(FP8X4),
                         rhs_scale=scales[:, g, ts],
@@ -177,8 +215,9 @@ def tile_lstmp_peephole_step_f1_kernel(
 
         def turn_cp(c):
             bank = t_tile([P, M], BF16, "cp_bank")
+            ci, c0 = chunk_of(cp_chunks, c)
             for t in range(4):
-                nc.tensor.transpose(bank[:, P * t : P * (t + 1)], cp[:, t, P * c : P * (c + 1)], ident_b[:])
+                nc.tensor.transpose(bank[:, P * t : P * (t + 1)], cp[ci][:, t, c0 : c0 + P], ident_b[:])
             return bank
 
         def keep_cp(c, bank):
@@ -242,7 +281,10 @@ def tile_lstmp_peephole_step_f1_kernel(
             if u == last:
                 return
             for t in range(4):
-                nc.sync.dma_start(out=hp[32 * j : 32 * j + 32, g, t, t0 : t0 + tn], in_=h[t:P:4, :])
+                nc.sync.dma_start(
+                    out=hp[32 * j : 32 * j + 32, g, t0 // 256 : (t0 + tn) // 256, t, :],
+                    in_=h[t:P:4, :].rearrange("p (a n) -> p a n", n=256),
+                )
 
         def s_act(u, key, src, func, gate):
             c, t0, tn = UNITS[u]
@@ -289,9 +331,9 @@ def tile_lstmp_peephole_step_f1_kernel(
                     in_=dst[:, rs, :],
                 )
 
-        def group_h(g, t0, tn, engine, p1=P):
-            dst = hg[0:p1, g, t0 : t0 + tn, :].rearrange("p (n i) t -> p n t i", i=4)
-            src = hp[0:p1, g, :, t0 : t0 + tn].rearrange("p t (n i) -> p n t i", i=4)
+        def group_h(g, t0, engine, p1=P):
+            dst = hg[0:p1, g, t0 : t0 + 256, :].rearrange("p (n i) t -> p n t i", i=4)
+            src = hp[0:p1, g, t0 // 256, :, :].rearrange("p t (n i) -> p n t i", i=4)
             if engine == "s":
                 nc.scalar.copy(out=dst, in_=src)
             else:
@@ -416,9 +458,9 @@ def tile_lstmp_peephole_step_f1_kernel(
             c, t0, tn = UNITS[u]
             step(u, finish_x if u == 0 else None, [c + 1] if 1 <= c < 7 else [])
             if u == 6:
-                group_h(0, 0, 256, "s")
+                group_h(0, 0, "s")
             if u == 7:
-                group_h(0, 256, 256, "s")
+                group_h(0, 256, "s")
                 quantize_h(0, 0, 256)
             if u == 8:
                 quantize_h(0, 256, 256)
@@ -426,13 +468,13 @@ def tile_lstmp_peephole_step_f1_kernel(
         v_uo(last)
         s_o(last)
         turn_c(last)
-        group_h(1, 256, 256, "v", 96)
+        group_h(1, 256, "v", 96)
         v_h(last)
         store_c(last)
         banks = [turn_h(256), turn_h(384)]
         untangle_h(256, banks[0], "v")
         untangle_h(384, banks[1], "s")
-        group_h(1, 0, 256, "v")
+        group_h(1, 0, "v")
         quantize_h(1, 256, 128)
         quantize_h(1, 384, 128)
         z = [project(2), project(3)]

@@ -20,7 +20,7 @@ ACT = mybir.ActivationFunctionType
 P = 128
 GI, GF, GA, GO = 0, 1, 2, 3
 
-ORDER = "xs0 xb0 xs1 rv0 rows xb1 w0 sx sr cp0 rv1 w1 w2 cp1 w3 cp2 wp"
+ORDER = "xs xb0 rv0 rows cp0 xb1 sx sr w0 rv1 w1 cp1 w2 cp2 w3 cp3 wp"
 UNITS = [(0, 0, 256), (0, 256, 256)] + [(c, 0, 512) for c in range(1, 7)] + [(7, 0, 256), (7, 256, 256)]
 
 
@@ -35,6 +35,7 @@ def tile_lstmp_peephole_step_f1_kernel(
 
         warm = keep.tile([P, 1], F32, name="warm")
         xs = keep.tile([P, K], F32, name="xs")
+        xs_col = keep.tile([P, 8], F32, name="xs_col")
         xb = keep.tile([P, 4, K], U8, name="xb")
         xv = keep.tile([P, 4, K], BF16, name="xv")
         rv = keep.tile([P, 4, R], BF16, name="rv")
@@ -50,7 +51,7 @@ def tile_lstmp_peephole_step_f1_kernel(
         pplanes = keep.tile([P, 2 * R], U8, name="pplanes", align_bytes=64)
         chunks = [(0, 128), (128, 256), (256, 512), (512, 1024)]
         words = [keep.tile([P, 3, 4, 2 * (b - a)], U8, name="words_%d" % a, align_bytes=64) for a, b in chunks]
-        cp_chunks = [(0, 128), (128, 512), (512, 1024)]
+        cp_chunks = [(0, 128), (128, 256), (256, 512), (512, 1024)]
         pwords = keep.tile([P, 2, 2 * R], U8, name="pwords", align_bytes=64)
         cp = [keep.tile([P, 4, b - a], BF16, name="cp_%d" % a) for a, b in cp_chunks]
         cpt = keep.tile([P, 8, M], BF16, name="cpt")
@@ -64,7 +65,6 @@ def tile_lstmp_peephole_step_f1_kernel(
         xb_src = x_bytes.rearrange("(t p) k -> p t k", p=P)
         rv_src = r_prev.rearrange("(t p) k -> p t k", p=P)
         cp_src = c_prev.rearrange("(t p) k -> p t k", p=P)
-        xs_row = x_scale.rearrange("o k -> (o k)")
         planes_i = planes[:].bitcast(I32)
         pplanes_i = pplanes[:].bitcast(I32)
         wx_s = wx_scales.bitcast(I32)
@@ -78,8 +78,8 @@ def tile_lstmp_peephole_step_f1_kernel(
         nc.gpsimd.tensor_copy(out=sel[:, :, 96:128], in_=ident_b[:].rearrange("p (i t) -> p t i", t=4))
         nc.gpsimd.memset(pplanes_i[:], 0)
         nc.vector.memset(rows[:], 0.0)
-        nc.vector.memset(planes_i[:, 0 : 2 * Q4], 0)
-        nc.vector.memset(planes_i[:, 2 * Q4 : 3 * Q4], 0)
+        for a in range(0, 3 * Q4, 512):
+            nc.vector.memset(planes_i[:, a : a + 512], 0)
 
         def load_words(i):
             a, b = chunks[i]
@@ -95,8 +95,8 @@ def tile_lstmp_peephole_step_f1_kernel(
             i = [k for k, (a, b) in enumerate(ranges) if a <= P * c < b][0]
             return i, P * c - ranges[i][0]
 
-        def load_xs(a, b):
-            nc.scalar.dma_start(out=xs[:, a:b], in_=xs_row[a:b].partition_broadcast(P))
+        def load_xs():
+            nc.sync.dma_start(out=xs_col[:], in_=x_scale.rearrange("o (n m) -> n (o m)", m=8))
 
         def load_xb(a, b):
             nc.sync.dma_start(out=xb[:, a:b, :], in_=xb_src[:, a:b, :])
@@ -129,8 +129,7 @@ def tile_lstmp_peephole_step_f1_kernel(
             nc.sync.dma_start(out=pwords[:], in_=wp_words.rearrange("g p n -> p g n"))
 
         loads = {
-            "xs0": lambda: load_xs(0, 512),
-            "xs1": lambda: load_xs(512, 1024),
+            "xs": load_xs,
             "xb0": lambda: load_xb(0, 2),
             "xb1": lambda: load_xb(2, 4),
             "rv0": lambda: load_rv(0, 2),
@@ -146,6 +145,7 @@ def tile_lstmp_peephole_step_f1_kernel(
             "cp0": lambda: load_cp(0),
             "cp1": lambda: load_cp(1),
             "cp2": lambda: load_cp(2),
+            "cp3": lambda: load_cp(3),
             "wp": load_projection,
         }
         for name in ORDER.split():
@@ -168,6 +168,18 @@ def tile_lstmp_peephole_step_f1_kernel(
 
         def hs_col(c):
             return col(56 + c)
+
+        def spread_scales(i, engine):
+            bank = z_tile([P, 4, P], F32, "xs_bank")
+            for j in range(4):
+                m = 4 * i + j
+                nc.tensor.transpose(bank[:, j, :], xs_col[:, m : m + 1].to_broadcast([P, P]), ident_f[:])
+            dst = xs[:].rearrange("p (n m) -> p n m", m=8)[:, :, 4 * i : 4 * i + 4]
+            src = bank[:].rearrange("p m n -> p n m")
+            if engine == "s":
+                nc.scalar.copy(out=dst, in_=src)
+            else:
+                nc.vector.tensor_copy(out=dst, in_=src)
 
         def product(t, g):
             ks = slice(512 * g, 512 * g + 512)
@@ -384,10 +396,13 @@ def tile_lstmp_peephole_step_f1_kernel(
                 nc.vector.tensor_copy(out=r_sb[:], in_=z[:])
             else:
                 nc.scalar.copy(out=r_sb[:], in_=z[:])
-            nc.sync.dma_start(out=out_r[P * t : P * (t + 1), :], in_=r_sb[:])
+            queue = nc.scalar if engine == "s" else nc.sync
+            queue.dma_start(out=out_r[P * t : P * (t + 1), :], in_=r_sb[:])
 
         ctx.enter_context(tc.manual_schedule(engines={mybir.EngineType.PE, mybir.EngineType.DVE, mybir.EngineType.Activation}))
 
+        spread_scales(0, "v")
+        spread_scales(1, "s")
         product(0, 0)
         product(1, 0)
         r0 = turn(rv, 2, 0, 0)
@@ -401,62 +416,64 @@ def tile_lstmp_peephole_step_f1_kernel(
         rows_bank = t_tile([P, P], BF16, "rows_bank")
         nc.tensor.transpose(rows_bank[:], rows[:], ident_b[:])
         nc.scalar.copy(out=cols[:], in_=rows_bank[:, 0:64])
+        b0 = turn_cp(0)
+        keep_cp(0, b0)
         product(2, 0)
-        product(3, 0)
         quantize(2, 0)
         quantize(0, 0)
         quantize(1, 0)
-        x10 = turn(xv, 0, 0, 1)
-        untangle(x10, 0, 1)
-        product(2, 1)
-        product(3, 1)
+        product(3, 0)
         matmuls(0, (GF, GI))
-        b0 = turn_cp(0)
-        keep_cp(0, b0)
-        matmuls(0, (GA, GO))
         r1 = turn(rv, 2, 0, 1)
         untangle(r1, 2, 1)
+        v_uf(0)
+        v_ui(0)
+        x10 = turn(xv, 0, 0, 1)
+        untangle(x10, 0, 1)
+        matmuls(0, (GA, GO))
+        product(2, 1)
+        product(3, 1)
+        s_f(0)
+        s_i(0)
+        s_a(0)
         x11 = turn(xv, 1, 256, 1)
         untangle(x11, 1, 1)
         b1 = turn_cp(1)
+        keep_cp(1, b1)
+        quantize(2, 1)
+        quantize(0, 1)
+        v_fc(0)
+        quantize(1, 1)
+        matmuls(1)
+        v_ia(0)
+        v_c(0)
 
-        def step(u, before=None, turns=()):
+        def step(u, turns):
             v_uf(u)
             s_a(u)
             v_ui(u)
-            if u > 0:
-                s_tanh(u - 1)
+            s_tanh(u - 1)
             s_f(u)
             s_i(u)
-            if before is not None:
-                before()
             if u < last:
                 matmuls(u + 1, (GF, GI))
-            if u > 0:
-                turn_c(u - 1)
-                v_uo(u - 1)
-                s_o(u - 1)
+            turn_c(u - 1)
+            v_uo(u - 1)
+            s_o(u - 1)
             banks = [(c, turn_cp(c)) for c in turns]
             if u < last:
                 matmuls(u + 1, (GA, GO))
             v_fc(u)
             v_ia(u)
-            if u > 0:
-                v_h(u - 1)
-                store_c(u - 1)
+            v_h(u - 1)
+            store_c(u - 1)
             v_c(u)
             for c, bank in banks:
                 keep_cp(c, bank)
 
-        def finish_x():
-            quantize(2, 1)
-            quantize(0, 1)
-            quantize(1, 1)
-            keep_cp(1, b1)
-
-        for u in range(last + 1):
+        for u in range(1, last + 1):
             c, t0, tn = UNITS[u]
-            step(u, finish_x if u == 0 else None, [c + 1] if 1 <= c < 7 else [])
+            step(u, [c + 1] if 1 <= c < 7 else [])
             if u == 6:
                 group_h(0, 0, "s")
             if u == 7:

@@ -20,7 +20,7 @@ ACT = mybir.ActivationFunctionType
 P = 128
 GI, GF, GA, GO = 0, 1, 2, 3
 
-ORDER = "xs xb0 rv0 rows cp0 xb1 sx sr w0 rv1 w1 cp1 w2 cp2 w3 cp3 wp"
+ORDER = "xs rv0 rows xb0 cp0 xb1 sx w0 sr rv1 w1 cp1 w2 cp2 wp"
 UNITS = [(0, 0, 256), (0, 256, 256)] + [(c, 0, 512) for c in range(1, 7)] + [(7, 0, 256), (7, 256, 256)]
 
 
@@ -35,6 +35,7 @@ def tile_lstmp_peephole_step_f1_kernel(
 
         warm = keep.tile([P, 1], F32, name="warm")
         xs = keep.tile([P, K], F32, name="xs")
+        zeros = keep.tile([P, 512], BF16, name="zeros")
         xs_col = keep.tile([P, 8], F32, name="xs_col")
         xb = keep.tile([P, 4, K], U8, name="xb")
         xv = keep.tile([P, 4, K], BF16, name="xv")
@@ -49,9 +50,9 @@ def tile_lstmp_peephole_step_f1_kernel(
         sel = keep.tile([P, 4, P], BF16, name="sel")
         planes = keep.tile([P, 3 * 4 * N], U8, name="planes", align_bytes=64)
         pplanes = keep.tile([P, 2 * R], U8, name="pplanes", align_bytes=64)
-        chunks = [(0, 128), (128, 256), (256, 512), (512, 1024)]
+        chunks = [(0, 128), (128, 512), (512, 1024)]
         words = [keep.tile([P, 3, 4, 2 * (b - a)], U8, name="words_%d" % a, align_bytes=64) for a, b in chunks]
-        cp_chunks = [(0, 128), (128, 256), (256, 512), (512, 1024)]
+        cp_chunks = [(0, 128), (128, 512), (512, 1024)]
         pwords = keep.tile([P, 2, 2 * R], U8, name="pwords", align_bytes=64)
         cp = [keep.tile([P, 4, b - a], BF16, name="cp_%d" % a) for a, b in cp_chunks]
         cpt = keep.tile([P, 8, M], BF16, name="cpt")
@@ -60,11 +61,12 @@ def tile_lstmp_peephole_step_f1_kernel(
         hcodes = keep.tile([P, 2, M], U32, name="hcodes", align_bytes=64)
         hscales = keep.tile([P, 2, M], U8, name="hscales", align_bytes=64)
 
+        nc.vector.memset(zeros[:], 0.0)
         nc.vector.memset(warm[:], 0.0)
         nc.scalar.activation(out=warm[:], in_=warm[:], func=ACT.Sigmoid)
-        xb_src = x_bytes.rearrange("(t p) k -> p t k", p=P)
-        rv_src = r_prev.rearrange("(t p) k -> p t k", p=P)
-        cp_src = c_prev.rearrange("(t p) k -> p t k", p=P)
+        xb_src = x_bytes.rearrange("(p t) k -> p t k", p=P)
+        rv_src = r_prev.rearrange("(p t) k -> p t k", p=P)
+        cp_src = c_prev.rearrange("(p t) k -> p t k", p=P)
         planes_i = planes[:].bitcast(I32)
         pplanes_i = pplanes[:].bitcast(I32)
         wx_s = wx_scales.bitcast(I32)
@@ -141,11 +143,9 @@ def tile_lstmp_peephole_step_f1_kernel(
             "w0": lambda: load_words(0),
             "w1": lambda: load_words(1),
             "w2": lambda: load_words(2),
-            "w3": lambda: load_words(3),
             "cp0": lambda: load_cp(0),
             "cp1": lambda: load_cp(1),
             "cp2": lambda: load_cp(2),
-            "cp3": lambda: load_cp(3),
             "wp": load_projection,
         }
         for name in ORDER.split():
@@ -180,6 +180,10 @@ def tile_lstmp_peephole_step_f1_kernel(
                 nc.scalar.copy(out=dst, in_=src)
             else:
                 nc.vector.tensor_copy(out=dst, in_=src)
+
+        def keep_warm(count):
+            for j in range(count):
+                nc.tensor.matmul(out=warm_bank[:], lhsT=zeros[:, 0:P], rhs=zeros[:], start=True, stop=True)
 
         def product(t, g):
             ks = slice(512 * g, 512 * g + 512)
@@ -245,25 +249,30 @@ def tile_lstmp_peephole_step_f1_kernel(
         def matmuls(u, gates=(GF, GI, GA, GO)):
             c, t0, tn = UNITS[u]
             for gate in gates:
-                state.setdefault(u, {})[gate] = gate_matmuls(gate, c, t0, tn)
+                if c < 7:
+                    state.setdefault(u, {})[gate] = gate_matmuls(gate, c, t0, tn)[:]
+                elif t0 == 0:
+                    z = gate_matmuls(gate, c, 0, M)
+                    for v in range(u, last + 1):
+                        state.setdefault(v, {})[gate] = z[:, UNITS[v][1] : UNITS[v][1] + UNITS[v][2]]
 
         def v_uf(u):
             c, t0, tn = UNITS[u]
             st = state[u]
             st["uf"] = w_tile("uf", tn)
-            nc.vector.scalar_tensor_tensor(out=st["uf"][:], in0=cpt[:, c, t0 : t0 + tn], scalar=peep_col(1, c), in1=st[GF][:], op0=ALU.mult, op1=ALU.add)
+            nc.vector.scalar_tensor_tensor(out=st["uf"][:], in0=cpt[:, c, t0 : t0 + tn], scalar=peep_col(1, c), in1=st[GF], op0=ALU.mult, op1=ALU.add)
 
         def v_ui(u):
             c, t0, tn = UNITS[u]
             st = state[u]
             st["ui"] = w_tile("ui", tn)
-            nc.vector.scalar_tensor_tensor(out=st["ui"][:], in0=cpt[:, c, t0 : t0 + tn], scalar=peep_col(0, c), in1=st[GI][:], op0=ALU.mult, op1=ALU.add)
+            nc.vector.scalar_tensor_tensor(out=st["ui"][:], in0=cpt[:, c, t0 : t0 + tn], scalar=peep_col(0, c), in1=st[GI], op0=ALU.mult, op1=ALU.add)
 
         def v_uo(u):
             c, t0, tn = UNITS[u]
             st = state[u]
             st["uo"] = w_tile("uo", tn)
-            nc.vector.scalar_tensor_tensor(out=st["uo"][:], in0=st["c"][:], scalar=peep_col(2, c), in1=st[GO][:], op0=ALU.mult, op1=ALU.add)
+            nc.vector.scalar_tensor_tensor(out=st["uo"][:], in0=st["c"][:], scalar=peep_col(2, c), in1=st[GO], op0=ALU.mult, op1=ALU.add)
 
         def v_fc(u):
             c, t0, tn = UNITS[u]
@@ -280,17 +289,17 @@ def tile_lstmp_peephole_step_f1_kernel(
         def v_c(u):
             c, t0, tn = UNITS[u]
             st = state[u]
-            st["c"] = w_tile("cn", tn, bufs=3)
+            st["c"] = w_tile("cn", tn, bufs=4)
             nc.vector.tensor_tensor(out=st["c"][:], in0=st["fc"][:], in1=st["ia"][:], op=ALU.add)
 
         def v_h(u):
             c, t0, tn = UNITS[u]
             st = state[u]
-            h = w_tile("h", tn, BF16, bufs=3)
+            h = w_tile("h", tn, BF16, bufs=len(UNITS))
             nc.vector.scalar_tensor_tensor(out=h[:], in0=st["o"][:], scalar=hs_col(c), in1=st["tanh"][:], op0=ALU.mult, op1=ALU.mult)
             st["h"] = h
             g, j = c // 4, c % 4
-            if u == last:
+            if c == 7:
                 return
             for t in range(4):
                 nc.sync.dma_start(
@@ -302,7 +311,7 @@ def tile_lstmp_peephole_step_f1_kernel(
             c, t0, tn = UNITS[u]
             st = state[u]
             st[key] = w_tile(key, tn)
-            nc.scalar.activation(out=st[key][:], in_=st[src][:], func=func, bias=bias_col(gate, c))
+            nc.scalar.activation(out=st[key][:], in_=st[src] if src == GA else st[src][:], func=func, bias=bias_col(gate, c))
 
         def s_a(u):
             s_act(u, "a", GA, ACT.Tanh, GA)
@@ -332,14 +341,14 @@ def tile_lstmp_peephole_step_f1_kernel(
         def store_c(u):
             c, t0, tn = UNITS[u]
             rs = slice(t0 // P, (t0 + tn) // P)
-            if c % 2 == 0 and t0 == 0:
-                c_rows[0] = work.tile([P, 4, 2 * P], F32, name="c_rows", tag="c_rows", bufs=2)
-            dst = c_rows[0]
+            if c // 2 not in c_rows:
+                c_rows[c // 2] = work.tile([P, 4, 2 * P], F32, name="c_rows", tag="c_rows", bufs=4)
+            dst = c_rows[c // 2]
             a = P * (c % 2)
             nc.scalar.copy(out=dst[:, rs, a : a + P], in_=state[u]["bank"][:])
             if c % 2 == 1:
                 nc.sync.dma_start(
-                    out=out_c.rearrange("(t p) n -> p t n", p=P)[:, rs, P * (c - 1) : P * (c + 1)],
+                    out=out_c.rearrange("(p t) n -> p t n", p=P)[:, rs, P * (c - 1) : P * (c + 1)],
                     in_=dst[:, rs, :],
                 )
 
@@ -351,10 +360,9 @@ def tile_lstmp_peephole_step_f1_kernel(
             else:
                 nc.vector.tensor_copy(out=dst, in_=src)
 
-        def turn_h(t0):
-            h = state[last]["h"]
-            a = t0 - UNITS[last][1]
-            bank = t_tile([P, 4, P], BF16, "h_bank")
+        def turn_h(u, a):
+            h = state[u]["h"]
+            bank = z_tile([P, 4, P], BF16, "h_bank")
             for t in range(4):
                 nc.tensor.matmul(out=bank[:, t, :], lhsT=sel[:, t, :], rhs=h[:, a : a + P], start=True, stop=True)
             return bank
@@ -397,18 +405,23 @@ def tile_lstmp_peephole_step_f1_kernel(
             else:
                 nc.scalar.copy(out=r_sb[:], in_=z[:])
             queue = nc.scalar if engine == "s" else nc.sync
-            queue.dma_start(out=out_r[P * t : P * (t + 1), :], in_=r_sb[:])
+            queue.dma_start(out=out_r.rearrange("(p t) n -> p t n", p=P)[:, t, :], in_=r_sb[:])
 
         ctx.enter_context(tc.manual_schedule(engines={mybir.EngineType.PE, mybir.EngineType.DVE, mybir.EngineType.Activation}))
 
+        warm_bank = z_tile([P, 512], F32, "warm_bank")
+        keep_warm(4)
         spread_scales(0, "v")
         spread_scales(1, "s")
+        keep_warm(2)
         product(0, 0)
         product(1, 0)
         r0 = turn(rv, 2, 0, 0)
         untangle(r0, 2, 0)
+        keep_warm(2)
         x00 = turn(xv, 0, 0, 0)
         untangle(x00, 0, 0)
+        keep_warm(1)
         product(0, 1)
         product(1, 1)
         x01 = turn(xv, 1, 256, 0)
@@ -418,86 +431,108 @@ def tile_lstmp_peephole_step_f1_kernel(
         nc.scalar.copy(out=cols[:], in_=rows_bank[:, 0:64])
         b0 = turn_cp(0)
         keep_cp(0, b0)
+        keep_warm(4)
         product(2, 0)
         quantize(2, 0)
         quantize(0, 0)
         quantize(1, 0)
         product(3, 0)
-        matmuls(0, (GF, GI))
-        r1 = turn(rv, 2, 0, 1)
-        untangle(r1, 2, 1)
-        v_uf(0)
-        v_ui(0)
         x10 = turn(xv, 0, 0, 1)
         untangle(x10, 0, 1)
-        matmuls(0, (GA, GO))
+        keep_warm(1)
         product(2, 1)
         product(3, 1)
-        s_f(0)
-        s_i(0)
-        s_a(0)
+        matmuls(0, (GF, GI))
         x11 = turn(xv, 1, 256, 1)
+        v_uf(0)
+        s_f(0)
         untangle(x11, 1, 1)
-        b1 = turn_cp(1)
-        keep_cp(1, b1)
-        quantize(2, 1)
         quantize(0, 1)
+        v_ui(0)
+        s_i(0)
+        matmuls(0, (GA,))
+        s_a(0)
+        r1 = turn(rv, 2, 0, 1)
+        untangle(r1, 2, 1)
+        matmuls(0, (GO,))
         v_fc(0)
         quantize(1, 1)
-        matmuls(1)
         v_ia(0)
-        v_c(0)
+        quantize(2, 1)
+        turned = {0}
 
-        def step(u, turns):
-            v_uf(u)
-            s_a(u)
-            v_ui(u)
-            s_tanh(u - 1)
-            s_f(u)
-            s_i(u)
-            if u < last:
-                matmuls(u + 1, (GF, GI))
-            turn_c(u - 1)
-            v_uo(u - 1)
-            s_o(u - 1)
-            banks = [(c, turn_cp(c)) for c in turns]
-            if u < last:
-                matmuls(u + 1, (GA, GO))
-            v_fc(u)
-            v_ia(u)
-            v_h(u - 1)
-            store_c(u - 1)
+        def step(u):
+            more = u < last
+            if more:
+                matmuls(u + 1, (GF,))
+            if u > 0:
+                v_fc(u)
+                v_ia(u)
+            if more:
+                v_uf(u + 1)
+                s_f(u + 1)
             v_c(u)
+            s_tanh(u)
+            if more:
+                matmuls(u + 1, (GA, GI))
+                s_a(u + 1)
+            if u > 0:
+                v_h(u - 1)
+            if more:
+                v_ui(u + 1)
+                s_i(u + 1)
+            if u > 0:
+                matmuls(u, (GO,))
+                turn_c(u - 1)
+            banks = []
+            c = UNITS[min(u + 2, last)][0]
+            if c not in turned:
+                turned.add(c)
+                banks.append((c, turn_cp(c)))
+            if 0 < u < last - 1:
+                store_c(u - 1)
+            v_uo(u)
             for c, bank in banks:
                 keep_cp(c, bank)
+            s_o(u)
+            if u == last - 1:
+                store_c(u - 1)
 
-        for u in range(1, last + 1):
-            c, t0, tn = UNITS[u]
-            step(u, [c + 1] if 1 <= c < 7 else [])
-            if u == 6:
+        for u in range(last):
+            step(u)
+            if u == 5:
                 group_h(0, 0, "s")
-            if u == 7:
+            if u == 6:
                 group_h(0, 256, "s")
                 quantize_h(0, 0, 256)
-            if u == 8:
+            if u == 7:
                 quantize_h(0, 256, 256)
+        v_fc(last)
+        v_ia(last)
+        v_h(last - 1)
+        turn_c(last - 1)
+        banks = [turn_h(last - 1, 0), turn_h(last - 1, 128)]
+        v_c(last)
         s_tanh(last)
+        turn_c(last)
         v_uo(last)
         s_o(last)
-        turn_c(last)
-        group_h(1, 256, "v", 96)
+        untangle_h(0, banks[0], "s")
+        untangle_h(128, banks[1], "s")
         v_h(last)
-        store_c(last)
-        banks = [turn_h(256), turn_h(384)]
-        untangle_h(256, banks[0], "v")
+        store_c(last - 1)
+        banks = [turn_h(last, 0), turn_h(last, 128)]
+        group_h(1, 0, "v", 96)
+        untangle_h(256, banks[0], "s")
+        quantize_h(1, 0, 256)
         untangle_h(384, banks[1], "s")
-        group_h(1, 0, "v")
+        group_h(1, 256, "v", 96)
+        store_c(last)
+        z = [project(0), project(1)]
         quantize_h(1, 256, 128)
         quantize_h(1, 384, 128)
-        z = [project(2), project(3)]
-        quantize_h(1, 0, 256)
-        store_r(2, z[0], "s")
-        store_r(3, z[1], "v")
-        z = [project(0), project(1)]
+        z = z + [project(2), project(3)]
         store_r(0, z[0], "v")
         store_r(1, z[1], "s")
+        store_r(2, z[2], "v")
+        store_r(3, z[3], "s")

@@ -20,8 +20,8 @@ ACT = mybir.ActivationFunctionType
 P = 128
 GI, GF, GA, GO = 0, 1, 2, 3
 
-ORDER = "xs rv0 rows xb0 cp0 xb1 sx w0 sr rv1 w1 cp1 w2 cp2 wp"
-UNITS = [(0, 0, 256), (0, 256, 256)] + [(c, 0, 512) for c in range(1, 7)] + [(7, 0, 256), (7, 256, 256)]
+ORDER = "xs xb0 xb1 rv rows sx w0 cp0 sr w1 cp1 w2 wp"
+UNITS = [(c, 0, 512) for c in range(7)] + [(7, 0, 256), (7, 256, 256)]
 
 
 def tile_lstmp_peephole_step_f1_kernel(
@@ -52,7 +52,7 @@ def tile_lstmp_peephole_step_f1_kernel(
         pplanes = keep.tile([P, 2 * R], U8, name="pplanes", align_bytes=64)
         chunks = [(0, 128), (128, 512), (512, 1024)]
         words = [keep.tile([P, 3, 4, 2 * (b - a)], U8, name="words_%d" % a, align_bytes=64) for a, b in chunks]
-        cp_chunks = [(0, 128), (128, 512), (512, 1024)]
+        cp_chunks = [(0, 256), (256, 1024)]
         pwords = keep.tile([P, 2, 2 * R], U8, name="pwords", align_bytes=64)
         cp = [keep.tile([P, 4, b - a], BF16, name="cp_%d" % a) for a, b in cp_chunks]
         cpt = keep.tile([P, 8, M], BF16, name="cpt")
@@ -145,7 +145,6 @@ def tile_lstmp_peephole_step_f1_kernel(
             "w2": lambda: load_words(2),
             "cp0": lambda: load_cp(0),
             "cp1": lambda: load_cp(1),
-            "cp2": lambda: load_cp(2),
             "wp": load_projection,
         }
         for name in ORDER.split():
@@ -169,14 +168,17 @@ def tile_lstmp_peephole_step_f1_kernel(
         def hs_col(c):
             return col(56 + c)
 
-        def spread_scales(i, engine):
+        def spread_scales(i):
             bank = z_tile([P, 4, P], F32, "xs_bank")
             for j in range(4):
                 m = 4 * i + j
                 nc.tensor.transpose(bank[:, j, :], xs_col[:, m : m + 1].to_broadcast([P, P]), ident_f[:])
-            dst = xs[:].rearrange("p (n m) -> p n m", m=8)[:, :, 4 * i : 4 * i + 4]
-            src = bank[:].rearrange("p m n -> p n m")
-            if engine == "s":
+            return bank
+
+        def keep_scales(i, bank, part):
+            dst = xs[:].rearrange("p (n m) -> p n m", m=8)[:, 64 * part : 64 * part + 64, 4 * i : 4 * i + 4]
+            src = bank[:, :, 64 * part : 64 * part + 64].rearrange("p m n -> p n m")
+            if part == 1:
                 nc.scalar.copy(out=dst, in_=src)
             else:
                 nc.vector.tensor_copy(out=dst, in_=src)
@@ -202,8 +204,8 @@ def tile_lstmp_peephole_step_f1_kernel(
             dst = dst.rearrange("p (i r u) -> p i r u", i=2, u=2)
             nc.scalar.copy(out=dst, in_=bank[:].rearrange("p i u r -> p i r u"))
 
-        def quantize(g, half):
-            ts = slice(256 * half, 256 * half + 256)
+        def quantize(g, t0, tn):
+            ts = slice(t0, t0 + tn)
             nc.vector.quantize_mx(
                 out=codes[:, g, ts].bitcast(FP8X4),
                 scales=scales[:, g, ts],
@@ -217,7 +219,7 @@ def tile_lstmp_peephole_step_f1_kernel(
             step = 512 if tn == 512 else 128
             for s0 in range(0, tn, step):
                 ts = slice(t0 + s0, t0 + s0 + step)
-                for j, g in enumerate((2, 0, 1)):
+                for j, g in enumerate((0, 2, 1)):
                     nc.tensor.matmul_mx(
                         out=z[:, s0 : s0 + step],
                         lhsT=words[wi][:, g, gate, 2 * w0 : 2 * (w0 + P)].bitcast(FP4X4),
@@ -341,20 +343,22 @@ def tile_lstmp_peephole_step_f1_kernel(
         def store_c(u):
             c, t0, tn = UNITS[u]
             rs = slice(t0 // P, (t0 + tn) // P)
-            if c // 2 not in c_rows:
-                c_rows[c // 2] = work.tile([P, 4, 2 * P], F32, name="c_rows", tag="c_rows", bufs=4)
-            dst = c_rows[c // 2]
-            a = P * (c % 2)
+            pair = c if c >= 6 else c // 2
+            if pair not in c_rows:
+                c_rows[pair] = work.tile([P, 4, 2 * P], F32, name="c_rows", tag="c_rows", bufs=5)
+            dst = c_rows[pair]
+            a = 0 if c >= 6 else P * (c % 2)
             nc.scalar.copy(out=dst[:, rs, a : a + P], in_=state[u]["bank"][:])
-            if c % 2 == 1:
+            if c >= 6 or c % 2 == 1:
                 nc.sync.dma_start(
-                    out=out_c.rearrange("(p t) n -> p t n", p=P)[:, rs, P * (c - 1) : P * (c + 1)],
-                    in_=dst[:, rs, :],
+                    out=out_c.rearrange("(p t) n -> p t n", p=P)[:, rs, P * c - a : P * (c + 1)],
+                    in_=dst[:, rs, 0 : a + P],
                 )
 
-        def group_h(g, t0, engine, p1=P):
-            dst = hg[0:p1, g, t0 : t0 + 256, :].rearrange("p (n i) t -> p n t i", i=4)
-            src = hp[0:p1, g, t0 // 256, :, :].rearrange("p t (n i) -> p n t i", i=4)
+        def group_h(g, t0, tn, engine, p1=P):
+            dst = hg[0:p1, g, t0 : t0 + tn, :].rearrange("p (n i) t -> p n t i", i=4)
+            a = t0 % 256
+            src = hp[0:p1, g, t0 // 256, :, a : a + tn].rearrange("p t (n i) -> p n t i", i=4)
             if engine == "s":
                 nc.scalar.copy(out=dst, in_=src)
             else:
@@ -404,62 +408,62 @@ def tile_lstmp_peephole_step_f1_kernel(
                 nc.vector.tensor_copy(out=r_sb[:], in_=z[:])
             else:
                 nc.scalar.copy(out=r_sb[:], in_=z[:])
-            queue = nc.scalar if engine == "s" else nc.sync
-            queue.dma_start(out=out_r.rearrange("(p t) n -> p t n", p=P)[:, t, :], in_=r_sb[:])
+            nc.sync.dma_start(out=out_r.rearrange("(p t) n -> p t n", p=P)[:, t, :], in_=r_sb[:])
 
         ctx.enter_context(tc.manual_schedule(engines={mybir.EngineType.PE, mybir.EngineType.DVE, mybir.EngineType.Activation}))
 
         warm_bank = z_tile([P, 512], F32, "warm_bank")
         keep_warm(4)
-        spread_scales(0, "v")
-        spread_scales(1, "s")
-        keep_warm(2)
+        xs_banks = [spread_scales(0), spread_scales(1)]
+        keep_scales(0, xs_banks[0], 0)
+        keep_scales(1, xs_banks[1], 1)
+        keep_scales(1, xs_banks[1], 0)
+        keep_scales(0, xs_banks[0], 1)
+        keep_warm(3)
         product(0, 0)
         product(1, 0)
-        r0 = turn(rv, 2, 0, 0)
-        untangle(r0, 2, 0)
-        keep_warm(2)
         x00 = turn(xv, 0, 0, 0)
         untangle(x00, 0, 0)
-        keep_warm(1)
+        product(2, 0)
+        product(3, 0)
+        r0 = turn(rv, 2, 0, 0)
+        untangle(r0, 2, 0)
+        x10 = turn(xv, 0, 0, 1)
+        untangle(x10, 0, 1)
+        r1 = turn(rv, 2, 0, 1)
+        untangle(r1, 2, 1)
         product(0, 1)
         product(1, 1)
         x01 = turn(xv, 1, 256, 0)
         untangle(x01, 1, 0)
-        rows_bank = t_tile([P, P], BF16, "rows_bank")
+        keep_warm(4)
+        product(2, 1)
+        product(3, 1)
+        x11 = turn(xv, 1, 256, 1)
+        untangle(x11, 1, 1)
+        keep_warm(1)
+        quantize(2, 0, 512)
+        quantize(0, 0, 512)
+        rows_bank = z_tile([P, P], BF16, "rows_bank")
         nc.tensor.transpose(rows_bank[:], rows[:], ident_b[:])
         nc.scalar.copy(out=cols[:], in_=rows_bank[:, 0:64])
         b0 = turn_cp(0)
+        b1 = turn_cp(1)
         keep_cp(0, b0)
-        keep_warm(4)
-        product(2, 0)
-        quantize(2, 0)
-        quantize(0, 0)
-        quantize(1, 0)
-        product(3, 0)
-        x10 = turn(xv, 0, 0, 1)
-        untangle(x10, 0, 1)
-        keep_warm(1)
-        product(2, 1)
-        product(3, 1)
+        keep_cp(1, b1)
+        quantize(1, 0, 256)
+        quantize(1, 256, 256)
         matmuls(0, (GF, GI))
-        x11 = turn(xv, 1, 256, 1)
         v_uf(0)
         s_f(0)
-        untangle(x11, 1, 1)
-        quantize(0, 1)
         v_ui(0)
         s_i(0)
         matmuls(0, (GA,))
         s_a(0)
-        r1 = turn(rv, 2, 0, 1)
-        untangle(r1, 2, 1)
         matmuls(0, (GO,))
         v_fc(0)
-        quantize(1, 1)
         v_ia(0)
-        quantize(2, 1)
-        turned = {0}
+        turned = {0, 1}
 
         def step(u):
             more = u < last
@@ -500,13 +504,10 @@ def tile_lstmp_peephole_step_f1_kernel(
 
         for u in range(last):
             step(u)
-            if u == 5:
-                group_h(0, 0, "s")
-            if u == 6:
-                group_h(0, 256, "s")
-                quantize_h(0, 0, 256)
+            if u in (4, 5, 6, 7):
+                group_h(0, 128 * (u - 4), 128, "s")
             if u == 7:
-                quantize_h(0, 256, 256)
+                quantize_h(0, 0, 256)
         v_fc(last)
         v_ia(last)
         v_h(last - 1)
@@ -519,20 +520,21 @@ def tile_lstmp_peephole_step_f1_kernel(
         s_o(last)
         untangle_h(0, banks[0], "s")
         untangle_h(128, banks[1], "s")
+        quantize_h(0, 256, 256)
         v_h(last)
         store_c(last - 1)
         banks = [turn_h(last, 0), turn_h(last, 128)]
-        group_h(1, 0, "v", 96)
+        group_h(1, 0, 256, "v", 96)
         untangle_h(256, banks[0], "s")
         quantize_h(1, 0, 256)
         untangle_h(384, banks[1], "s")
-        group_h(1, 256, "v", 96)
+        group_h(1, 256, 256, "v", 96)
         store_c(last)
         z = [project(0), project(1)]
         quantize_h(1, 256, 128)
         quantize_h(1, 384, 128)
         z = z + [project(2), project(3)]
-        store_r(0, z[0], "v")
+        store_r(0, z[0], "s")
         store_r(1, z[1], "s")
         store_r(2, z[2], "v")
         store_r(3, z[3], "s")

from contextlib import ExitStack

import concourse.mybir as mybir
from concourse.masks import make_identity

M, K, R, N = 512, 1024, 512, 1024
FLOPS = 2 * M * (K + R) * 4 * N + 2 * M * N * R

F32 = mybir.dt.float32
BF16 = mybir.dt.bfloat16
U32 = mybir.dt.uint32
I32 = mybir.dt.int32
U8 = mybir.dt.uint8
FP8 = mybir.dt.float8_e4m3fn
FP8X4 = mybir.dt.float8_e4m3fn_x4
FP4X4 = mybir.dt.float4_e2m1fn_x4
ALU = mybir.AluOpType
ACT = mybir.ActivationFunctionType

P = 128
GI, GF, GA, GO = 0, 1, 2, 3

ORDER = "xs xb0 xb1 rv rows sx w0 cp0 sr w1 cp1 w2 wp"
UNITS = [(c, 0, 512) for c in range(7)] + [(7, 0, 256), (7, 256, 256)]


def tile_lstmp_peephole_step_f1_kernel(
    tc, x_bytes, x_scale, r_prev, c_prev, wx_words, wx_scales, wr_words, wr_scales, bias, peep, hscale, wp_words, wp_scales, out_r, out_c
):
    nc = tc.nc
    with ExitStack() as ctx:
        keep = ctx.enter_context(tc.tile_pool(name="keep", bufs=1))
        work = ctx.enter_context(tc.tile_pool(name="work", bufs=2))
        psum = ctx.enter_context(tc.psum_pool(name="psum", bufs=1))

        warm = keep.tile([P, 1], F32, name="warm")
        xs = keep.tile([P, K], F32, name="xs")
        zeros = keep.tile([P, 512], BF16, name="zeros")
        xs_col = keep.tile([P, 8], F32, name="xs_col")
        xb = keep.tile([P, 4, K], U8, name="xb")
        xv = keep.tile([P, 4, K], BF16, name="xv")
        rv = keep.tile([P, 4, R], BF16, name="rv")
        grouped = keep.tile([P, 3, M, 4], BF16, name="grouped", align_bytes=64)
        codes = keep.tile([P, 3, M], U32, name="codes", align_bytes=64)
        scales = keep.tile([P, 3, M], U8, name="scales", align_bytes=64)
        rows = keep.tile([P, P], BF16, name="rows")
        cols = keep.tile([P, 64], F32, name="cols")
        ident_f = keep.tile([P, P], F32, name="ident_f")
        ident_b = keep.tile([P, P], BF16, name="ident_b")
        sel = keep.tile([P, 4, P], BF16, name="sel")
        planes = keep.tile([P, 3 * 4 * N], U8, name="planes", align_bytes=64)
        pplanes = keep.tile([P, 2 * R], U8, name="pplanes", align_bytes=64)
        chunks = [(0, 128), (128, 512), (512, 1024)]
        words = [keep.tile([P, 3, 4, 2 * (b - a)], U8, name="words_%d" % a, align_bytes=64) for a, b in chunks]
        cp_chunks = [(0, 256), (256, 1024)]
        pwords = keep.tile([P, 2, 2 * R], U8, name="pwords", align_bytes=64)
        cp = [keep.tile([P, 4, b - a], BF16, name="cp_%d" % a) for a, b in cp_chunks]
        cpt = keep.tile([P, 8, M], BF16, name="cpt")
        hp = keep.tile([P, 2, 2, 4, 256], BF16, name="hp")
        hg = keep.tile([P, 2, M, 4], BF16, name="hg", align_bytes=64)
        hcodes = keep.tile([P, 2, M], U32, name="hcodes", align_bytes=64)
        hscales = keep.tile([P, 2, M], U8, name="hscales", align_bytes=64)

        nc.vector.memset(zeros[:], 0.0)
        nc.vector.memset(warm[:], 0.0)
        nc.scalar.activation(out=warm[:], in_=warm[:], func=ACT.Sigmoid)
        xb_src = x_bytes.rearrange("(p t) k -> p t k", p=P)
        rv_src = r_prev.rearrange("(p t) k -> p t k", p=P)
        cp_src = c_prev.rearrange("(p t) k -> p t k", p=P)
        planes_i = planes[:].bitcast(I32)
        pplanes_i = pplanes[:].bitcast(I32)
        wx_s = wx_scales.bitcast(I32)
        wr_s = wr_scales.bitcast(I32)
        wp_s = wp_scales.bitcast(I32)
        Q4 = N

        make_identity(nc, ident_f[:])
        make_identity(nc, ident_b[:])
        nc.gpsimd.memset(sel[:], 0.0)
        nc.gpsimd.tensor_copy(out=sel[:, :, 96:128], in_=ident_b[:].rearrange("p (i t) -> p t i", t=4))
        nc.gpsimd.memset(pplanes_i[:], 0)
        nc.vector.memset(rows[:], 0.0)
        for a in range(0, 3 * Q4, 512):
            nc.vector.memset(planes_i[:, a : a + 512], 0)

        def load_words(i):
            a, b = chunks[i]
            for g in (2, 0, 1):
                src = wr_words[0] if g == 2 else wx_words[g]
                nc.sync.dma_start(out=words[i][:, g, :, :], in_=src.rearrange("p (q n) -> p q n", q=4)[:, :, 2 * a : 2 * b])

        def load_cp(i):
            a, b = cp_chunks[i]
            nc.sync.dma_start(out=cp[i][:], in_=cp_src[:, :, a:b])

        def chunk_of(ranges, c):
            i = [k for k, (a, b) in enumerate(ranges) if a <= P * c < b][0]
            return i, P * c - ranges[i][0]

        def load_xs():
            nc.sync.dma_start(out=xs_col[:], in_=x_scale.rearrange("o (n m) -> n (o m)", m=8))

        def load_xb(a, b):
            nc.sync.dma_start(out=xb[:, a:b, :], in_=xb_src[:, a:b, :])

        def load_rv(a, b):
            nc.sync.dma_start(out=rv[:, a:b, :], in_=rv_src[:, a:b, :])

        def load_rows():
            nc.sync.dma_start(out=rows[0:32, :], in_=bias.rearrange("(a b) -> a b", b=P))
            nc.sync.dma_start(out=rows[32:56, :], in_=peep.rearrange("g (a b) -> (g a) b", b=P))
            nc.sync.dma_start(out=rows[56:64, :], in_=hscale.rearrange("(a b) -> a b", b=P))

        def load_wx_scales():
            for r in range(4):
                nc.sync.dma_start(
                    out=planes_i[r:P:32, 0 : 2 * Q4].rearrange("p (g n) -> p g n", g=2),
                    in_=wx_s[:, r:16:4, :].rearrange("g q n -> q g n"),
                )

        def load_wr_scales():
            for r in range(4):
                nc.sync.dma_start(out=planes_i[r:P:32, 2 * Q4 : 3 * Q4], in_=wr_s[0, r:16:4, :])

        def load_projection():
            for r in range(4):
                nc.sync.dma_start(
                    out=pplanes_i[r:P:32, :].rearrange("p (g n) -> p g n", g=2),
                    in_=wp_s[:, r:16:4, :].rearrange("g q n -> q g n"),
                )
            nc.sync.dma_start(out=pwords[:], in_=wp_words.rearrange("g p n -> p g n"))

        loads = {
            "xs": load_xs,
            "xb0": lambda: load_xb(0, 2),
            "xb1": lambda: load_xb(2, 4),
            "rv0": lambda: load_rv(0, 2),
            "rv1": lambda: load_rv(2, 4),
            "rv": lambda: load_rv(0, 4),
            "rows": load_rows,
            "sx": load_wx_scales,
            "sr": load_wr_scales,
            "w0": lambda: load_words(0),
            "w1": lambda: load_words(1),
            "w2": lambda: load_words(2),
            "cp0": lambda: load_cp(0),
            "cp1": lambda: load_cp(1),
            "wp": load_projection,
        }
        for name in ORDER.split():
            loads[name]()

        def z_tile(shape, dtype, name):
            return psum.tile(shape, dtype, name=name, tag="z", bufs=6)

        def t_tile(shape, dtype, name):
            return psum.tile(shape, dtype, name=name, tag="t", bufs=2)

        def col(i):
            return cols[:, i : i + 1]

        def bias_col(gate, c):
            return col(8 * gate + c)

        def peep_col(j, c):
            return col(32 + 8 * j + c)

        def hs_col(c):
            return col(56 + c)

        def spread_scales(i):
            bank = z_tile([P, 4, P], F32, "xs_bank")
            for j in range(4):
                m = 4 * i + j
                nc.tensor.transpose(bank[:, j, :], xs_col[:, m : m + 1].to_broadcast([P, P]), ident_f[:])
            return bank

        def keep_scales(i, bank, part):
            dst = xs[:].rearrange("p (n m) -> p n m", m=8)[:, 64 * part : 64 * part + 64, 4 * i : 4 * i + 4]
            src = bank[:, :, 64 * part : 64 * part + 64].rearrange("p m n -> p n m")
            if part == 1:
                nc.scalar.copy(out=dst, in_=src)
            else:
                nc.vector.tensor_copy(out=dst, in_=src)

        def keep_warm(count):
            for j in range(count):
                nc.tensor.matmul(out=warm_bank[:], lhsT=zeros[:, 0:P], rhs=zeros[:], start=True, stop=True)

        def product(t, g):
            ks = slice(512 * g, 512 * g + 512)
            nc.vector.tensor_tensor(out=xv[:, t, ks], in0=xb[:, t, ks].bitcast(FP8), in1=xs[:, ks], op=ALU.mult)

        def turn(src, g, word0, half):
            bank = z_tile([P, 2, 2, P], F32, "turn")
            for i in range(2):
                w = src[:, 2 * half + i, :].bitcast(F32)
                for u in range(2):
                    nc.tensor.transpose(bank[:, i, u, :], w[:, word0 + u : word0 + 256 : 2], ident_f[:])
            return bank

        def untangle(bank, g, half):
            dst = grouped[:, g, 256 * half : 256 * half + 256, :].rearrange("p n t -> p (n t)").bitcast(F32)
            dst = dst.rearrange("p (i r u) -> p i r u", i=2, u=2)
            nc.scalar.copy(out=dst, in_=bank[:].rearrange("p i u r -> p i r u"))

        def quantize(g, t0, tn):
            ts = slice(t0, t0 + tn)
            nc.vector.quantize_mx(
                out=codes[:, g, ts].bitcast(FP8X4),
                scales=scales[:, g, ts],
                in_=grouped[:, g, ts, :].rearrange("p n t -> p (n t)"),
            )

        def gate_matmuls(gate, c, t0, tn):
            z = z_tile([P, tn], F32, "z")
            n0 = gate * N + P * c
            wi, w0 = chunk_of(chunks, c)
            step = 512 if tn == 512 else 128
            for s0 in range(0, tn, step):
                ts = slice(t0 + s0, t0 + s0 + step)
                for j, g in enumerate((0, 2, 1)):
                    nc.tensor.matmul_mx(
                        out=z[:, s0 : s0 + step],
                        lhsT=words[wi][:, g, gate, 2 * w0 : 2 * (w0 + P)].bitcast(FP4X4),
                        lhsT_scale=planes[:, g * 4 * N + n0 : g * 4 * N + n0 + P],
                        rhs=codes[:, g, ts].bitcast(FP8X4),
                        rhs_scale=scales[:, g, ts],
                        start=(j == 0),
                        stop=(j == 2),
                    )
            return z

        def turn_cp(c):
            bank = t_tile([P, M], BF16, "cp_bank")
            ci, c0 = chunk_of(cp_chunks, c)
            for t in range(4):
                nc.tensor.transpose(bank[:, P * t : P * (t + 1)], cp[ci][:, t, c0 : c0 + P], ident_b[:])
            return bank

        def keep_cp(c, bank):
            nc.scalar.copy(out=cpt[:, c, :], in_=bank[:])

        def w_tile(name, tn, dtype=F32, bufs=2):
            return work.tile([P, tn], dtype, name=name, tag=name, bufs=bufs)

        state = {}
        c_rows = {}
        last = len(UNITS) - 1

        def matmuls(u, gates=(GF, GI, GA, GO)):
            c, t0, tn = UNITS[u]
            for gate in gates:
                if c < 7:
                    state.setdefault(u, {})[gate] = gate_matmuls(gate, c, t0, tn)[:]
                elif t0 == 0:
                    z = gate_matmuls(gate, c, 0, M)
                    for v in range(u, last + 1):
                        state.setdefault(v, {})[gate] = z[:, UNITS[v][1] : UNITS[v][1] + UNITS[v][2]]

        def v_uf(u):
            c, t0, tn = UNITS[u]
            st = state[u]
            st["uf"] = w_tile("uf", tn)
            nc.vector.scalar_tensor_tensor(out=st["uf"][:], in0=cpt[:, c, t0 : t0 + tn], scalar=peep_col(1, c), in1=st[GF], op0=ALU.mult, op1=ALU.add)

        def v_ui(u):
            c, t0, tn = UNITS[u]
            st = state[u]
            st["ui"] = w_tile("ui", tn)
            nc.vector.scalar_tensor_tensor(out=st["ui"][:], in0=cpt[:, c, t0 : t0 + tn], scalar=peep_col(0, c), in1=st[GI], op0=ALU.mult, op1=ALU.add)

        def v_uo(u):
            c, t0, tn = UNITS[u]
            st = state[u]
            st["uo"] = w_tile("uo", tn)
            nc.vector.scalar_tensor_tensor(out=st["uo"][:], in0=st["c"][:], scalar=peep_col(2, c), in1=st[GO], op0=ALU.mult, op1=ALU.add)

        def v_fc(u):
            c, t0, tn = UNITS[u]
            st = state[u]
            st["fc"] = w_tile("fc", tn)
            nc.vector.tensor_tensor(out=st["fc"][:], in0=st["f"][:], in1=cpt[:, c, t0 : t0 + tn], op=ALU.mult)

        def v_ia(u):
            c, t0, tn = UNITS[u]
            st = state[u]
            st["ia"] = w_tile("ia", tn)
            nc.vector.tensor_tensor(out=st["ia"][:], in0=st["i"][:], in1=st["a"][:], op=ALU.mult)

        def v_c(u):
            c, t0, tn = UNITS[u]
            st = state[u]
            st["c"] = w_tile("cn", tn, bufs=4)
            nc.vector.tensor_tensor(out=st["c"][:], in0=st["fc"][:], in1=st["ia"][:], op=ALU.add)

        def v_h(u):
            c, t0, tn = UNITS[u]
            st = state[u]
            h = w_tile("h", tn, BF16, bufs=len(UNITS))
            nc.vector.scalar_tensor_tensor(out=h[:], in0=st["o"][:], scalar=hs_col(c), in1=st["tanh"][:], op0=ALU.mult, op1=ALU.mult)
            st["h"] = h
            g, j = c // 4, c % 4
            if c == 7:
                return
            for t in range(4):
                nc.sync.dma_start(
                    out=hp[32 * j : 32 * j + 32, g, t0 // 256 : (t0 + tn) // 256, t, :],
                    in_=h[t:P:4, :].rearrange("p (a n) -> p a n", n=256),
                )

        def s_act(u, key, src, func, gate):
            c, t0, tn = UNITS[u]
            st = state[u]
            st[key] = w_tile(key, tn)
            nc.scalar.activation(out=st[key][:], in_=st[src] if src == GA else st[src][:], func=func, bias=bias_col(gate, c))

        def s_a(u):
            s_act(u, "a", GA, ACT.Tanh, GA)

        def s_f(u):
            s_act(u, "f", "uf", ACT.Sigmoid, GF)

        def s_i(u):
            s_act(u, "i", "ui", ACT.Sigmoid, GI)

        def s_o(u):
            s_act(u, "o", "uo", ACT.Sigmoid, GO)

        def s_tanh(u):
            c, t0, tn = UNITS[u]
            st = state[u]
            st["tanh"] = w_tile("tanh", tn)
            nc.scalar.activation(out=st["tanh"][:], in_=st["c"][:], func=ACT.Tanh)

        def turn_c(u):
            c, t0, tn = UNITS[u]
            bank = t_tile([P, tn // P, P], F32, "c_bank")
            for i in range(tn // P):
                nc.tensor.transpose(bank[:, i, :], state[u]["c"][:, P * i : P * (i + 1)], ident_f[:])
            state[u]["bank"] = bank

        def store_c(u):
            c, t0, tn = UNITS[u]
            rs = slice(t0 // P, (t0 + tn) // P)
            pair = c if c >= 6 else c // 2
            if pair not in c_rows:
                c_rows[pair] = work.tile([P, 4, 2 * P], F32, name="c_rows", tag="c_rows", bufs=5)
            dst = c_rows[pair]
            a = 0 if c >= 6 else P * (c % 2)
            nc.scalar.copy(out=dst[:, rs, a : a + P], in_=state[u]["bank"][:])
            if c >= 6 or c % 2 == 1:
                nc.sync.dma_start(
                    out=out_c.rearrange("(p t) n -> p t n", p=P)[:, rs, P * c - a : P * (c + 1)],
                    in_=dst[:, rs, 0 : a + P],
                )

        def group_h(g, t0, tn, engine, p1=P):
            dst = hg[0:p1, g, t0 : t0 + tn, :].rearrange("p (n i) t -> p n t i", i=4)
            a = t0 % 256
            src = hp[0:p1, g, t0 // 256, :, a : a + tn].rearrange("p t (n i) -> p n t i", i=4)
            if engine == "s":
                nc.scalar.copy(out=dst, in_=src)
            else:
                nc.vector.tensor_copy(out=dst, in_=src)

        def turn_h(u, a):
            h = state[u]["h"]
            bank = z_tile([P, 4, P], BF16, "h_bank")
            for t in range(4):
                nc.tensor.matmul(out=bank[:, t, :], lhsT=sel[:, t, :], rhs=h[:, a : a + P], start=True, stop=True)
            return bank

        def untangle_h(t0, bank, engine):
            dst = hg[96:P, 1, t0 : t0 + P, :]
            src = bank[96:P, :, :].rearrange("p t n -> p n t")
            if engine == "s":
                nc.scalar.copy(out=dst, in_=src)
            else:
                nc.vector.tensor_copy(out=dst, in_=src)

        def quantize_h(g, t0, tn):
            ts = slice(t0, t0 + tn)
            nc.vector.quantize_mx(
                out=hcodes[:, g, ts].bitcast(FP8X4),
                scales=hscales[:, g, ts],
                in_=hg[:, g, ts, :].rearrange("p n t -> p (n t)"),
            )

        def project(t):
            z = z_tile([P, R], F32, "r")
            ts = slice(P * t, P * (t + 1))
            for g in range(2):
                nc.tensor.matmul_mx(
                    out=z[:],
                    lhsT=hcodes[:, g, ts].bitcast(FP8X4),
                    lhsT_scale=hscales[:, g, ts],
                    rhs=pwords[:, g, :].bitcast(FP4X4),
                    rhs_scale=pplanes[:, g * R : (g + 1) * R],
                    start=(g == 0),
                    stop=(g == 1),
                )
            return z

        def store_r(t, z, engine):
            r_sb = work.tile([P, R], F32, name="r_sb", tag="r_sb", bufs=4)
            if engine == "v":
                nc.vector.tensor_copy(out=r_sb[:], in_=z[:])
            else:
                nc.scalar.copy(out=r_sb[:], in_=z[:])
            nc.sync.dma_start(out=out_r.rearrange("(p t) n -> p t n", p=P)[:, t, :], in_=r_sb[:])

        ctx.enter_context(tc.manual_schedule(engines={mybir.EngineType.PE, mybir.EngineType.DVE, mybir.EngineType.Activation}))

        warm_bank = z_tile([P, 512], F32, "warm_bank")
        keep_warm(4)
        xs_banks = [spread_scales(0), spread_scales(1)]
        keep_scales(0, xs_banks[0], 0)
        keep_scales(1, xs_banks[1], 1)
        keep_scales(1, xs_banks[1], 0)
        keep_scales(0, xs_banks[0], 1)
        keep_warm(3)
        product(0, 0)
        product(1, 0)
        x00 = turn(xv, 0, 0, 0)
        untangle(x00, 0, 0)
        product(2, 0)
        product(3, 0)
        r0 = turn(rv, 2, 0, 0)
        untangle(r0, 2, 0)
        x10 = turn(xv, 0, 0, 1)
        untangle(x10, 0, 1)
        r1 = turn(rv, 2, 0, 1)
        untangle(r1, 2, 1)
        product(0, 1)
        product(1, 1)
        x01 = turn(xv, 1, 256, 0)
        untangle(x01, 1, 0)
        keep_warm(4)
        product(2, 1)
        product(3, 1)
        x11 = turn(xv, 1, 256, 1)
        untangle(x11, 1, 1)
        keep_warm(1)
        quantize(2, 0, 512)
        quantize(0, 0, 512)
        rows_bank = z_tile([P, P], BF16, "rows_bank")
        nc.tensor.transpose(rows_bank[:], rows[:], ident_b[:])
        nc.scalar.copy(out=cols[:], in_=rows_bank[:, 0:64])
        b0 = turn_cp(0)
        b1 = turn_cp(1)
        keep_cp(0, b0)
        keep_cp(1, b1)
        quantize(1, 0, 256)
        quantize(1, 256, 256)
        matmuls(0, (GF, GI))
        v_uf(0)
        s_f(0)
        v_ui(0)
        s_i(0)
        matmuls(0, (GA,))
        s_a(0)
        matmuls(0, (GO,))
        v_fc(0)
        v_ia(0)
        turned = {0, 1}

        def step(u):
            more = u < last
            if more:
                matmuls(u + 1, (GF,))
            if u > 0:
                v_fc(u)
                v_ia(u)
            if more:
                v_uf(u + 1)
                s_f(u + 1)
            v_c(u)
            s_tanh(u)
            if more:
                matmuls(u + 1, (GA, GI))
                s_a(u + 1)
            if u > 0:
                v_h(u - 1)
            if more:
                v_ui(u + 1)
                s_i(u + 1)
            if u > 0:
                matmuls(u, (GO,))
                turn_c(u - 1)
            banks = []
            c = UNITS[min(u + 2, last)][0]
            if c not in turned:
                turned.add(c)
                banks.append((c, turn_cp(c)))
            if 0 < u < last - 1:
                store_c(u - 1)
            v_uo(u)
            for c, bank in banks:
                keep_cp(c, bank)
            s_o(u)
            if u == last - 1:
                store_c(u - 1)

        for u in range(last):
            step(u)
            if u in (4, 5, 6, 7):
                group_h(0, 128 * (u - 4), 128, "s")
            if u == 7:
                quantize_h(0, 0, 256)
        v_fc(last)
        v_ia(last)
        v_h(last - 1)
        turn_c(last - 1)
        banks = [turn_h(last - 1, 0), turn_h(last - 1, 128)]
        v_c(last)
        s_tanh(last)
        turn_c(last)
        v_uo(last)
        s_o(last)
        untangle_h(0, banks[0], "s")
        untangle_h(128, banks[1], "s")
        quantize_h(0, 256, 256)
        v_h(last)
        store_c(last - 1)
        banks = [turn_h(last, 0), turn_h(last, 128)]
        group_h(1, 0, 256, "v", 96)
        untangle_h(256, banks[0], "s")
        quantize_h(1, 0, 256)
        untangle_h(384, banks[1], "s")
        group_h(1, 256, 256, "v", 96)
        store_c(last)
        z = [project(0), project(1)]
        quantize_h(1, 256, 128)
        quantize_h(1, 384, 128)
        z = z + [project(2), project(3)]
        store_r(0, z[0], "s")
        store_r(1, z[1], "s")
        store_r(2, z[2], "v")
        store_r(3, z[3], "s")
